import numpy as np
import ml_dtypes


def mxq(x, axis, fmt="e4m3"):
    dtype, down = {"e4m3": (ml_dtypes.float8_e4m3fn, 7), "e5m2": (ml_dtypes.float8_e5m2, 14)}[fmt]
    v = np.moveaxis(np.asarray(x, np.float32).astype(ml_dtypes.bfloat16).astype(np.float64), axis, -1)
    blocks = v.reshape(v.shape[:-1] + (-1, 32))
    amax = np.abs(blocks).max(-1, keepdims=True)
    byte = np.maximum(np.where(amax > 0, np.frexp(amax)[1] - 1 + 127, 0) - down, 1)
    scale = np.exp2(byte - 127.0)
    codes = (blocks / scale).astype(np.float32).astype(dtype).astype(np.float64)
    return np.moveaxis((codes * scale).reshape(v.shape), -1, axis)


WIDE = False


def mx_kscale(k):
    if not WIDE:
        return np.ones(k)
    levels = np.array([10, -10, 5, -5, 0])
    if k % 512:
        return np.exp2(np.random.permutation(np.resize(levels, k // 32))).repeat(32)
    a = np.empty((k // 512, 16))
    for p in range(k // 512):
        a[p, :8] = np.random.permutation(np.resize(levels, 8))
        for g in range(8):
            far = levels[np.abs(levels - a[p, g]) >= 10]
            a[p, g + 8] = far[np.random.randint(len(far))]
    return np.exp2(a.ravel()).repeat(32)


def f64(x):
    return np.asarray(x).astype(np.float64)


def striped(idx):
    return np.tile(idx.reshape(-1, 16).T, (8, 1)).astype(np.uint16)


def unstriped(offs):
    return offs[:16].T.reshape(-1).astype(np.int64)


def striped8(idx):
    return np.concatenate([x.reshape(-1, 16).T for x in idx]).astype(np.uint16)


def runs(offs, k):
    lists = np.stack([offs[16 * r : 16 * r + 16].T.reshape(-1) for r in range(8)]).astype(np.int64)
    return lists[np.arange(k) % 512 // 64]


def pack_weight(w):
    k, n = w.shape
    w = f64(np.asarray(w, np.float32).astype(ml_dtypes.bfloat16)).reshape(k // 32, 32, n)
    amax = np.abs(w).max(1)
    byte = np.clip(np.where(amax > 0, np.frexp(amax)[1] - 1 + 127 - 7, 1), 1, 254)
    scaled = (w * np.exp2(127.0 - byte)[:, None, :]).reshape(k, n).astype(np.float32)
    words = np.ascontiguousarray(scaled.reshape(k // 512, 128, 4, n).transpose(0, 1, 3, 2)).astype(ml_dtypes.float8_e4m3fn).view(np.uint8)
    return words, np.ascontiguousarray(byte.astype(np.uint8).reshape(k // 512, 16, n))


def unpack_weight(words, scales):
    g, p, n, _ = words.shape
    vals = np.ascontiguousarray(words).view(ml_dtypes.float8_e4m3fn).astype(np.float64) * np.repeat(np.exp2(scales.astype(np.float64) - 127.0), 8, axis=1)[..., None]
    return vals.transpose(0, 1, 3, 2).reshape(g * 512, n)


K, T, S, V, N, H = 512, 2048, 512, 256, 512, 512


def setup_inputs():
    n = np.random.standard_normal
    s = mx_kscale(K)[:, None]
    u = mx_kscale(S)
    packed_xT = pack_weight(n((K, T)) * s)
    perm = np.stack([np.random.permutation(H) for _ in range(8)])
    return {
        "x_words": packed_xT[0],
        "x_scales": packed_xT[1],
        "wa": (n((K, H)) / np.sqrt(K) / s).astype(np.float32),
        "gt": (np.random.uniform(0.5, 1.5, (S, 1)) * u[:, None]).astype(np.float32),
        "w1": (n((S, N)) / np.sqrt(S) / u[:, None]).astype(np.float32),
        "offs": striped(np.random.permutation(T)[:S]),
        "la": striped8(perm[:, :V]),
        "lb": striped8(perm[:, V:]),
    }


def reference(x_words, x_scales, wa, gt, w1, offs, la, lb):
    xq = unpack_weight(x_words, x_scales)[:, unstriped(offs)]
    y = xq.T @ mxq(f64(wa), 0, "e4m3")
    a = y[np.arange(S)[:, None], runs(la, S)]
    b = y[np.arange(S)[:, None], runs(lb, S)]
    mx = np.maximum(a, b)
    mn = np.minimum(a, b)
    p = np.zeros((S, H))
    p[np.arange(S)[:, None], runs(la, S)] = mn
    zs = p.copy()
    zs[np.arange(S)[:, None], runs(lb, S)] = mx
    z = f64(gt) * zs
    return mxq(f64(w1), 0, "e4m3").T @ mxq(z, 0, "e4m3")

@@ -1,0 +1,139 @@
+from contextlib import ExitStack
+
+import concourse.mybir as mybir
+
+K, T, S, V, N, H = 512, 2048, 512, 256, 512, 512
+FLOPS = 2 * K * S * H + 2 * S * N * H
+
+F32 = mybir.dt.float32
+BF16 = mybir.dt.bfloat16
+I32 = mybir.dt.int32
+U32 = mybir.dt.uint32
+U16 = mybir.dt.uint16
+U8 = mybir.dt.uint8
+FP8X4 = mybir.dt.float8_e4m3fn_x4
+ALU = mybir.AluOpType
+COPY = mybir.ActivationFunctionType.Copy
+
+P = 128
+PACK = 4
+HALF = 256
+
+
+def interleave(copy, grouped, raw):
+    copy(
+        out=grouped.rearrange("p (c i) j -> p c j i", i=4),
+        in_=raw.rearrange("p j (c i) -> p c j i", i=4),
+    )
+
+
+def tile_picked_mixscat_none_p_kernel(tc, x_words, x_scales, wa, gt, w1, offs, la, lb, out):
+    nc = tc.nc
+    with ExitStack() as ctx:
+        keep = ctx.enter_context(tc.tile_pool(name="keep", bufs=1))
+        psum = ctx.enter_context(tc.psum_pool(name="psum", bufs=8))
+
+        offs_sb = keep.tile([P, S // 16], U16, name="offs_sb")
+        la_sb = keep.tile([P, V // 16], U16, name="la_sb")
+        lb_sb = keep.tile([P, V // 16], U16, name="lb_sb")
+        x_table = keep.tile([P, T], I32, name="x_table", tag="wide", align_bytes=64)
+        s_table = keep.tile([P, T], U8, name="s_table", tag="narrow", align_bytes=64)
+        wa_raw = [keep.tile([P, PACK, HALF], F32, name=f"wa_raw{h}", align_bytes=64) for h in range(2)]
+
+        nc.vector.memset(s_table[:].bitcast(I32), 0)
+        nc.sync.dma_start(offs_sb[:], offs)
+        nc.sync.dma_start(la_sb[:], la)
+        for q in range(4):
+            nc.scalar.dma_start(s_table[32 * q : 32 * q + 4, :].bitcast(I32), x_scales[0, 4 * q : 4 * q + 4, :].bitcast(I32))
+        wa_rows = wa.rearrange("(p j) n -> p j n", j=PACK)
+        nc.sync.dma_start(wa_raw[0][:], wa_rows[:, :, 0:HALF])
+        nc.sync.dma_start(x_table[:], x_words[0].rearrange("p n r -> p (n r)").bitcast(I32))
+        nc.sync.dma_start(wa_raw[1][:], wa_rows[:, :, HALF:H])
+        nc.sync.dma_start(lb_sb[:], lb)
+
+        x_codes = keep.tile([P, PACK, P], U32, name="x_codes", align_bytes=64)
+        nc.vector.tensor_copy(x_codes[:].rearrange("p t m -> p m t"), x_table[:].bitcast(U32).indirect(offs_sb[:]))
+        s_picked = keep.tile([P, S], U8, name="s_picked", align_bytes=64)
+        nc.vector.tensor_copy(s_picked[:], s_table[:].indirect(offs_sb[:]))
+        x_planes = keep.tile([P, PACK, P], U8, name="x_planes", align_bytes=64)
+        nc.vector.tensor_copy(x_planes[:], s_picked[:].rearrange("p (m t) -> p t m", t=PACK))
+
+        w1_raw = keep.tile([P, PACK, N], F32, name="w1_raw", tag="wide", align_bytes=64)
+        nc.sync.dma_start(w1_raw[:], w1.rearrange("(p j) n -> p j n", j=PACK))
+        gate = keep.tile([P, PACK], F32, name="gate", tag="narrow", align_bytes=64)
+        nc.sync.dma_start(gate[:], gt.rearrange("(p t) o -> p (t o)", t=PACK))
+
+        wa_codes = keep.tile([P, H], U32, name="wa_codes", align_bytes=64)
+        wa_plane = keep.tile([P, H], U8, name="wa_plane", align_bytes=64)
+        for h in range(2):
+            cols = slice(h * HALF, (h + 1) * HALF)
+            wa_bf = keep.tile([P, HALF, PACK], BF16, name=f"wa_bf{h}", align_bytes=64)
+            interleave(nc.scalar.copy, wa_bf[:], wa_raw[h][:])
+            nc.vector.quantize_mx(out=wa_codes[:, cols].bitcast(FP8X4), scales=wa_plane[:, cols], in_=wa_bf[:].rearrange("p n j -> p (n j)"))
+
+        y = [keep.tile([P, H], F32, name=f"y{t}", align_bytes=64) for t in range(PACK)]
+        for t in range(PACK):
+            pieces = [slice(0, HALF), slice(HALF, H)] if t == 0 else [slice(0, H)]
+            for i, cols in enumerate(pieces):
+                acc = psum.tile([P, cols.stop - cols.start], F32, name="acc")
+                nc.tensor.matmul_mx(
+                    out=acc[:],
+                    lhsT=x_codes[:, t, :].bitcast(FP8X4),
+                    lhsT_scale=x_planes[:, t, :],
+                    rhs=wa_codes[:, cols].bitcast(FP8X4),
+                    rhs_scale=wa_plane[:, cols],
+                    start=True,
+                    stop=True,
+                )
+                if t == 0 and i == 1:
+                    nc.vector.tensor_copy(y[t][:, cols], acc[:])
+                else:
+                    nc.scalar.copy(y[t][:, cols], acc[:])
+
+        z_bf = [keep.tile([P, HALF, PACK], BF16, name=f"z_bf{h}", align_bytes=64) for h in range(2)]
+        w1_codes = keep.tile([P, N], U32, name="w1_codes", align_bytes=64)
+        w1_plane = keep.tile([P, N], U8, name="w1_plane", align_bytes=64)
+        w1_bf = keep.tile([P, N, PACK], BF16, name="w1_bf", align_bytes=64)
+        for t in range(PACK):
+            a = keep.tile([P, V], F32, name=f"a{t}", align_bytes=64)
+            b = keep.tile([P, V], F32, name=f"b{t}", align_bytes=64)
+            lo = keep.tile([P, V], F32, name=f"lo{t}", align_bytes=64)
+            hi = keep.tile([P, V], F32, name=f"hi{t}", align_bytes=64)
+            zs = keep.tile([P, H], F32, name=f"zs{t}", align_bytes=64)
+            nc.vector.tensor_copy(a[:], y[t][:].indirect(la_sb[:]))
+            nc.vector.tensor_copy(b[:], y[t][:].indirect(lb_sb[:]))
+            nc.vector.tensor_tensor(lo[:], a[:], b[:], ALU.min)
+            nc.vector.tensor_tensor(hi[:], a[:], b[:], ALU.max)
+            nc.vector.tensor_copy(zs[:].indirect(la_sb[:]), lo[:])
+            nc.vector.tensor_copy(zs[:].indirect(lb_sb[:]), hi[:])
+            for h in range(2):
+                nc.scalar.activation(z_bf[h][:, :, t], zs[:, h * HALF : (h + 1) * HALF], COPY, scale=gate[:, t : t + 1])
+            if t == 0:
+                for m in range(N // P):
+                    cols = slice(m * P, (m + 1) * P)
+                    interleave(nc.scalar.copy, w1_bf[:, cols, :], w1_raw[:, :, cols])
+            if t == 2:
+                nc.vector.quantize_mx(out=w1_codes[:].bitcast(FP8X4), scales=w1_plane[:], in_=w1_bf[:].rearrange("p n j -> p (n j)"))
+
+        for h in range(2):
+            z_codes = keep.tile([P, HALF], U32, name=f"z_codes{h}", align_bytes=64)
+            z_plane = keep.tile([P, HALF], U8, name=f"z_plane{h}", align_bytes=64)
+            nc.vector.quantize_mx(out=z_codes[:].bitcast(FP8X4), scales=z_plane[:], in_=z_bf[h][:].rearrange("p n j -> p (n j)"))
+            for m in range(N // P):
+                rows = slice(m * P, (m + 1) * P)
+                acc = psum.tile([P, HALF], F32, name="acc")
+                nc.tensor.matmul_mx(
+                    out=acc[:],
+                    lhsT=w1_codes[:, rows].bitcast(FP8X4),
+                    lhsT_scale=w1_plane[:, rows],
+                    rhs=z_codes[:].bitcast(FP8X4),
+                    rhs_scale=z_plane[:],
+                    start=True,
+                    stop=True,
+                )
+                result = keep.tile([P, HALF], F32, name=f"result{h}{m}", align_bytes=64)
+                if m % 2 == 0:
+                    nc.vector.tensor_copy(result[:], acc[:])
+                else:
+                    nc.scalar.copy(result[:], acc[:])
+                nc.sync.dma_start(out[rows, h * HALF : (h + 1) * HALF], result[:])

@@ -40,85 +40,94 @@ def tile_picked_mixscat_none_p_kernel(tc, x_words, x_scales, wa, gt, w1, offs, l
         s_table = keep.tile([P, T], U8, name="s_table", tag="narrow", align_bytes=64)
         wa_raw = [keep.tile([P, PACK, HALF], F32, name=f"wa_raw{h}", align_bytes=64) for h in range(2)]
 
-        nc.vector.memset(s_table[:].bitcast(I32), 0)
+        s_rows = keep.tile([P, T // 4], I32, name="s_rows", align_bytes=64)
         nc.sync.dma_start(offs_sb[:], offs)
-        nc.sync.dma_start(la_sb[:], la)
         for q in range(4):
-            nc.scalar.dma_start(s_table[32 * q : 32 * q + 4, :].bitcast(I32), x_scales[0, 4 * q : 4 * q + 4, :].bitcast(I32))
-        wa_rows = wa.rearrange("(p j) n -> p j n", j=PACK)
-        nc.sync.dma_start(wa_raw[0][:], wa_rows[:, :, 0:HALF])
+            nc.sync.dma_start(s_rows[32 * q : 32 * q + 4, :], x_scales[0, 4 * q : 4 * q + 4, :].bitcast(I32))
         nc.sync.dma_start(x_table[:], x_words[0].rearrange("p n r -> p (n r)").bitcast(I32))
-        nc.sync.dma_start(wa_raw[1][:], wa_rows[:, :, HALF:H])
+        wa_rows = wa.rearrange("(p j) n -> p j n", j=PACK)
+        for h in range(2):
+            nc.sync.dma_start(wa_raw[h][:], wa_rows[:, :, h * HALF : (h + 1) * HALF])
+        nc.sync.dma_start(la_sb[:], la)
         nc.sync.dma_start(lb_sb[:], lb)
 
-        x_codes = keep.tile([P, PACK, P], U32, name="x_codes", align_bytes=64)
-        nc.vector.tensor_copy(x_codes[:].rearrange("p t m -> p m t"), x_table[:].bitcast(U32).indirect(offs_sb[:]))
+        nc.vector.memset(s_table[:].bitcast(I32), 0)
+        for q in range(4):
+            nc.vector.tensor_copy(s_table[32 * q : 32 * q + 4, :].bitcast(I32), s_rows[32 * q : 32 * q + 4, :])
         s_picked = keep.tile([P, S], U8, name="s_picked", align_bytes=64)
         nc.vector.tensor_copy(s_picked[:], s_table[:].indirect(offs_sb[:]))
-        x_planes = keep.tile([P, PACK, P], U8, name="x_planes", align_bytes=64)
-        nc.vector.tensor_copy(x_planes[:], s_picked[:].rearrange("p (m t) -> p t m", t=PACK))
+        x_codes = keep.tile([P, PACK, P], U32, name="x_codes", align_bytes=64)
+        nc.vector.tensor_copy(x_codes[:].rearrange("p t m -> p m t"), x_table[:].bitcast(U32).indirect(offs_sb[:]))
+        s_dealt = s_picked[:].rearrange("p (m t) -> p t m", t=PACK)
+        first_plane = keep.tile([P, P], U8, name="first_plane", align_bytes=64)
+        nc.vector.tensor_copy(first_plane[:], s_dealt[:, 0, :])
+
+        wa_codes = keep.tile([P, H], U32, name="wa_codes", align_bytes=64)
+        wa_plane = keep.tile([P, H], U8, name="wa_plane", align_bytes=64)
+        wa_bf = [keep.tile([P, HALF, PACK], BF16, name=f"wa_bf{h}", tag=f"wa_bf{h}", align_bytes=64) for h in range(2)]
+        interleave(nc.scalar.copy, wa_bf[0][:], wa_raw[0][:])
+        interleave(nc.scalar.copy, wa_bf[1][:, :P, :], wa_raw[1][:, :, :P])
+        interleave(nc.vector.tensor_copy, wa_bf[1][:, P:, :], wa_raw[1][:, :, P:])
+        for h in range(2):
+            cols = slice(h * HALF, (h + 1) * HALF)
+            nc.vector.quantize_mx(out=wa_codes[:, cols].bitcast(FP8X4), scales=wa_plane[:, cols], in_=wa_bf[h][:].rearrange("p n j -> p (n j)"))
+        other_planes = keep.tile([P, PACK - 1, P], U8, name="other_planes", tag="wa_bf1", align_bytes=64)
+        nc.vector.tensor_copy(other_planes[:], s_dealt[:, 1:, :])
+        x_planes = [first_plane[:]] + [other_planes[:, t, :] for t in range(PACK - 1)]
 
         w1_raw = keep.tile([P, PACK, N], F32, name="w1_raw", tag="wide", align_bytes=64)
         nc.sync.dma_start(w1_raw[:], w1.rearrange("(p j) n -> p j n", j=PACK))
         gate = keep.tile([P, PACK], F32, name="gate", tag="narrow", align_bytes=64)
         nc.sync.dma_start(gate[:], gt.rearrange("(p t) o -> p (t o)", t=PACK))
 
-        wa_codes = keep.tile([P, H], U32, name="wa_codes", align_bytes=64)
-        wa_plane = keep.tile([P, H], U8, name="wa_plane", align_bytes=64)
-        for h in range(2):
-            cols = slice(h * HALF, (h + 1) * HALF)
-            wa_bf = keep.tile([P, HALF, PACK], BF16, name=f"wa_bf{h}", align_bytes=64)
-            interleave(nc.scalar.copy, wa_bf[:], wa_raw[h][:])
-            nc.vector.quantize_mx(out=wa_codes[:, cols].bitcast(FP8X4), scales=wa_plane[:, cols], in_=wa_bf[:].rearrange("p n j -> p (n j)"))
 
-        y = [keep.tile([P, H], F32, name=f"y{t}", align_bytes=64) for t in range(PACK)]
+        y = [keep.tile([P, H], F32, name=f"y{t}", tag=f"y{t}", align_bytes=64) for t in range(PACK)]
         for t in range(PACK):
             pieces = [slice(0, HALF), slice(HALF, H)] if t == 0 else [slice(0, H)]
-            for i, cols in enumerate(pieces):
+            for cols in pieces:
                 acc = psum.tile([P, cols.stop - cols.start], F32, name="acc")
                 nc.tensor.matmul_mx(
                     out=acc[:],
                     lhsT=x_codes[:, t, :].bitcast(FP8X4),
-                    lhsT_scale=x_planes[:, t, :],
+                    lhsT_scale=x_planes[t],
                     rhs=wa_codes[:, cols].bitcast(FP8X4),
                     rhs_scale=wa_plane[:, cols],
                     start=True,
                     stop=True,
                 )
-                if t == 0 and i == 1:
-                    nc.vector.tensor_copy(y[t][:, cols], acc[:])
-                else:
-                    nc.scalar.copy(y[t][:, cols], acc[:])
+                nc.scalar.copy(y[t][:, cols], acc[:])
 
         z_bf = [keep.tile([P, HALF, PACK], BF16, name=f"z_bf{h}", align_bytes=64) for h in range(2)]
-        w1_codes = keep.tile([P, N], U32, name="w1_codes", align_bytes=64)
-        w1_plane = keep.tile([P, N], U8, name="w1_plane", align_bytes=64)
-        w1_bf = keep.tile([P, N, PACK], BF16, name="w1_bf", align_bytes=64)
+        a = keep.tile([P, PACK, V], F32, name="a", align_bytes=64)
+        b = keep.tile([P, PACK, V], F32, name="b", align_bytes=64)
         for t in range(PACK):
-            a = keep.tile([P, V], F32, name=f"a{t}", align_bytes=64)
-            b = keep.tile([P, V], F32, name=f"b{t}", align_bytes=64)
-            lo = keep.tile([P, V], F32, name=f"lo{t}", align_bytes=64)
-            hi = keep.tile([P, V], F32, name=f"hi{t}", align_bytes=64)
-            zs = keep.tile([P, H], F32, name=f"zs{t}", align_bytes=64)
-            nc.vector.tensor_copy(a[:], y[t][:].indirect(la_sb[:]))
-            nc.vector.tensor_copy(b[:], y[t][:].indirect(lb_sb[:]))
-            nc.vector.tensor_tensor(lo[:], a[:], b[:], ALU.min)
-            nc.vector.tensor_tensor(hi[:], a[:], b[:], ALU.max)
-            nc.vector.tensor_copy(zs[:].indirect(la_sb[:]), lo[:])
-            nc.vector.tensor_copy(zs[:].indirect(lb_sb[:]), hi[:])
-            for h in range(2):
-                nc.scalar.activation(z_bf[h][:, :, t], zs[:, h * HALF : (h + 1) * HALF], COPY, scale=gate[:, t : t + 1])
-            if t == 0:
-                for m in range(N // P):
-                    cols = slice(m * P, (m + 1) * P)
-                    interleave(nc.scalar.copy, w1_bf[:, cols, :], w1_raw[:, :, cols])
-            if t == 2:
-                nc.vector.quantize_mx(out=w1_codes[:].bitcast(FP8X4), scales=w1_plane[:], in_=w1_bf[:].rearrange("p n j -> p (n j)"))
+            nc.vector.tensor_copy(a[:, t, :], y[t][:].indirect(la_sb[:]))
+            nc.vector.tensor_copy(b[:, t, :], y[t][:].indirect(lb_sb[:]))
+        w1_bf = keep.tile([P, N, PACK], BF16, name="w1_bf", tag="y3", align_bytes=64)
+        interleave(nc.scalar.copy, w1_bf[:], w1_raw[:])
 
+        lo = keep.tile([P, PACK, V], F32, name="lo", align_bytes=64)
+        hi = keep.tile([P, PACK, V], F32, name="hi", tag="late", align_bytes=64)
+        nc.vector.tensor_tensor(lo[:], a[:], b[:], ALU.min)
+        nc.vector.tensor_tensor(hi[:], a[:], b[:], ALU.max)
+        zs = [keep.tile([P, H], F32, name=f"zs{t}", align_bytes=64) for t in range(PACK)]
+        for pair in ((0, 1), (2, 3)):
+            for t in pair:
+                nc.vector.tensor_copy(zs[t][:].indirect(la_sb[:]), lo[:, t, :])
+            for t in pair:
+                nc.vector.tensor_copy(zs[t][:].indirect(lb_sb[:]), hi[:, t, :])
+                for h in range(2):
+                    nc.scalar.activation(z_bf[h][:, :, t], zs[t][:, h * HALF : (h + 1) * HALF], COPY, scale=gate[:, t : t + 1])
+
+        w1_codes = keep.tile([P, N], U32, name="w1_codes", tag="late", align_bytes=64)
+        w1_plane = keep.tile([P, N], U8, name="w1_plane", align_bytes=64)
+        nc.vector.quantize_mx(out=w1_codes[:].bitcast(FP8X4), scales=w1_plane[:], in_=w1_bf[:].rearrange("p n j -> p (n j)"))
+
+        z_codes = [keep.tile([P, HALF], U32, name=f"z_codes{h}", align_bytes=64) for h in range(2)]
+        z_plane = [keep.tile([P, HALF], U8, name=f"z_plane{h}", align_bytes=64) for h in range(2)]
         for h in range(2):
-            z_codes = keep.tile([P, HALF], U32, name=f"z_codes{h}", align_bytes=64)
-            z_plane = keep.tile([P, HALF], U8, name=f"z_plane{h}", align_bytes=64)
-            nc.vector.quantize_mx(out=z_codes[:].bitcast(FP8X4), scales=z_plane[:], in_=z_bf[h][:].rearrange("p n j -> p (n j)"))
+            nc.vector.quantize_mx(out=z_codes[h][:].bitcast(FP8X4), scales=z_plane[h][:], in_=z_bf[h][:].rearrange("p n j -> p (n j)"))
+        for h in range(2):
             for m in range(N // P):
                 rows = slice(m * P, (m + 1) * P)
                 acc = psum.tile([P, HALF], F32, name="acc")
@@ -126,8 +135,8 @@ def tile_picked_mixscat_none_p_kernel(tc, x_words, x_scales, wa, gt, w1, offs, l
                     out=acc[:],
                     lhsT=w1_codes[:, rows].bitcast(FP8X4),
                     lhsT_scale=w1_plane[:, rows],
-                    rhs=z_codes[:].bitcast(FP8X4),
-                    rhs_scale=z_plane[:],
+                    rhs=z_codes[h][:].bitcast(FP8X4),
+                    rhs_scale=z_plane[h][:],
                     start=True,
                     stop=True,
                 )

@@ -43,7 +43,8 @@ def tile_picked_mixscat_none_p_kernel(tc, x_words, x_scales, wa, gt, w1, offs, l
         s_rows = keep.tile([P, T // 4], I32, name="s_rows", align_bytes=64)
         nc.sync.dma_start(offs_sb[:], offs)
         for q in range(4):
-            nc.sync.dma_start(s_rows[32 * q : 32 * q + 4, :], x_scales[0, 4 * q : 4 * q + 4, :].bitcast(I32))
+            queue = nc.sync if q < 2 else nc.scalar
+            queue.dma_start(s_rows[32 * q : 32 * q + 4, :], x_scales[0, 4 * q : 4 * q + 4, :].bitcast(I32))
         nc.sync.dma_start(x_table[:], x_words[0].rearrange("p n r -> p (n r)").bitcast(I32))
         wa_rows = wa.rearrange("(p j) n -> p j n", j=PACK)
         for h in range(2):

@@ -18,6 +18,8 @@ COPY = mybir.ActivationFunctionType.Copy
 P = 128
 PACK = 4
 HALF = 256
+SHARE = 256
+WA_CUT = (128, 96)
 
 
 def interleave(copy, grouped, raw):
@@ -38,7 +40,7 @@ def tile_picked_mixscat_none_p_kernel(tc, x_words, x_scales, wa, gt, w1, offs, l
         lb_sb = keep.tile([P, V // 16], U16, name="lb_sb")
         x_table = keep.tile([P, T], I32, name="x_table", tag="wide", align_bytes=64)
         s_table = keep.tile([P, T], U8, name="s_table", tag="narrow", align_bytes=64)
-        wa_raw = [keep.tile([P, PACK, HALF], F32, name=f"wa_raw{h}", align_bytes=64) for h in range(2)]
+        wa_raw = [keep.tile([P, PACK, HALF], F32, name=f"wa_raw{h}", tag=f"wa_raw{h}", align_bytes=64) for h in range(2)]
 
         s_rows = keep.tile([P, T // 4], I32, name="s_rows", align_bytes=64)
         nc.sync.dma_start(offs_sb[:], offs)
@@ -60,17 +62,18 @@ def tile_picked_mixscat_none_p_kernel(tc, x_words, x_scales, wa, gt, w1, offs, l
         x_codes = keep.tile([P, PACK, P], U32, name="x_codes", align_bytes=64)
         nc.vector.tensor_copy(x_codes[:].rearrange("p t m -> p m t"), x_table[:].bitcast(U32).indirect(offs_sb[:]))
         s_dealt = s_picked[:].rearrange("p (m t) -> p t m", t=PACK)
-        first_plane = keep.tile([P, P], U8, name="first_plane", align_bytes=64)
-        nc.vector.tensor_copy(first_plane[:], s_dealt[:, 0, :])
 
         wa_codes = keep.tile([P, H], U32, name="wa_codes", align_bytes=64)
         wa_plane = keep.tile([P, H], U8, name="wa_plane", align_bytes=64)
         wa_bf = [keep.tile([P, HALF, PACK], BF16, name=f"wa_bf{h}", tag=f"wa_bf{h}", align_bytes=64) for h in range(2)]
-        interleave(nc.scalar.copy, wa_bf[0][:], wa_raw[0][:])
-        interleave(nc.scalar.copy, wa_bf[1][:, :P, :], wa_raw[1][:, :, :P])
-        interleave(nc.vector.tensor_copy, wa_bf[1][:, P:, :], wa_raw[1][:, :, P:])
         for h in range(2):
             cols = slice(h * HALF, (h + 1) * HALF)
+            cut = WA_CUT[h]
+            interleave(nc.scalar.copy, wa_bf[h][:, :cut, :], wa_raw[h][:, :, :cut])
+            interleave(nc.vector.tensor_copy, wa_bf[h][:, cut:, :], wa_raw[h][:, :, cut:])
+            if h == 0:
+                first_plane = keep.tile([P, P], U8, name="first_plane", tag="wa_raw0", align_bytes=64)
+                nc.vector.tensor_copy(first_plane[:], s_dealt[:, 0, :])
             nc.vector.quantize_mx(out=wa_codes[:, cols].bitcast(FP8X4), scales=wa_plane[:, cols], in_=wa_bf[h][:].rearrange("p n j -> p (n j)"))
         other_planes = keep.tile([P, PACK - 1, P], U8, name="other_planes", tag="wa_bf1", align_bytes=64)
         nc.vector.tensor_copy(other_planes[:], s_dealt[:, 1:, :])
@@ -107,43 +110,73 @@ def tile_picked_mixscat_none_p_kernel(tc, x_words, x_scales, wa, gt, w1, offs, l
         w1_bf = keep.tile([P, N, PACK], BF16, name="w1_bf", tag="y3", align_bytes=64)
         interleave(nc.scalar.copy, w1_bf[:], w1_raw[:])
 
-        lo = keep.tile([P, PACK, V], F32, name="lo", align_bytes=64)
-        hi = keep.tile([P, PACK, V], F32, name="hi", tag="late", align_bytes=64)
-        nc.vector.tensor_tensor(lo[:], a[:], b[:], ALU.min)
+        lo = keep.tile([P, PACK, V], F32, name="lo", tag="lo", align_bytes=64)
+        hi = keep.tile([P, PACK, V], F32, name="hi", align_bytes=64)
+        nc.vector.tensor_tensor(lo[:, :3, :], a[:, :3, :], b[:, :3, :], ALU.min)
         nc.vector.tensor_tensor(hi[:], a[:], b[:], ALU.max)
-        zs = [keep.tile([P, H], F32, name=f"zs{t}", align_bytes=64) for t in range(PACK)]
+        nc.vector.tensor_tensor(lo[:, 3, :], a[:, 3, :], b[:, 3, :], ALU.min)
+        zs = [keep.tile([P, H], F32, name=f"zs{t}", tag=f"zs{t}", align_bytes=64) for t in range(PACK)]
+        last = PACK - 1
+        w1_codes = [keep.tile([P, HALF], U32, name=f"w1_codes{h}", tag=("lo", "zs2")[h], align_bytes=64) for h in range(2)]
+        w1_plane = [keep.tile([P, HALF], U8, name=f"w1_plane{h}", align_bytes=64) for h in range(2)]
+
+        def quantize_w1(h):
+            nc.vector.quantize_mx(out=w1_codes[h][:].bitcast(FP8X4), scales=w1_plane[h][:], in_=w1_bf[:, h * HALF : (h + 1) * HALF, :].rearrange("p n j -> p (n j)"))
+
         for pair in ((0, 1), (2, 3)):
             for t in pair:
                 nc.vector.tensor_copy(zs[t][:].indirect(la_sb[:]), lo[:, t, :])
             for t in pair:
                 nc.vector.tensor_copy(zs[t][:].indirect(lb_sb[:]), hi[:, t, :])
-                for h in range(2):
-                    nc.scalar.activation(z_bf[h][:, :, t], zs[t][:, h * HALF : (h + 1) * HALF], COPY, scale=gate[:, t : t + 1])
-
-        w1_codes = keep.tile([P, N], U32, name="w1_codes", tag="late", align_bytes=64)
-        w1_plane = keep.tile([P, N], U8, name="w1_plane", align_bytes=64)
-        nc.vector.quantize_mx(out=w1_codes[:].bitcast(FP8X4), scales=w1_plane[:], in_=w1_bf[:].rearrange("p n j -> p (n j)"))
+                scale = gate[:, t : t + 1]
+                if t == last - 1:
+                    nc.scalar.activation(z_bf[0][:, :, t:], zs[t][:, :HALF].unsqueeze(2).to_broadcast([P, HALF, 2]), COPY, scale=scale)
+                elif t == last:
+                    if SHARE < HALF:
+                        nc.scalar.activation(z_bf[0][:, SHARE:, t], zs[t][:, SHARE:HALF], COPY, scale=scale)
+                else:
+                    nc.scalar.activation(z_bf[0][:, :, t], zs[t][:, :HALF], COPY, scale=scale)
+                nc.scalar.activation(z_bf[1][:, :, t], zs[t][:, HALF:], COPY, scale=scale)
+        quantize_w1(0)
+        for c in (0, P):
+            nc.vector.tensor_scalar(z_bf[0][:, c : c + P, last], zs[last][:, c : c + P], gate[:, last:], None, ALU.mult)
 
         z_codes = [keep.tile([P, HALF], U32, name=f"z_codes{h}", align_bytes=64) for h in range(2)]
         z_plane = [keep.tile([P, HALF], U8, name=f"z_plane{h}", align_bytes=64) for h in range(2)]
-        for h in range(2):
-            nc.vector.quantize_mx(out=z_codes[h][:].bitcast(FP8X4), scales=z_plane[h][:], in_=z_bf[h][:].rearrange("p n j -> p (n j)"))
-        for h in range(2):
-            for m in range(N // P):
-                rows = slice(m * P, (m + 1) * P)
-                acc = psum.tile([P, HALF], F32, name="acc")
-                nc.tensor.matmul_mx(
-                    out=acc[:],
-                    lhsT=w1_codes[:, rows].bitcast(FP8X4),
-                    lhsT_scale=w1_plane[:, rows],
-                    rhs=z_codes[h][:].bitcast(FP8X4),
-                    rhs_scale=z_plane[h][:],
-                    start=True,
-                    stop=True,
-                )
-                result = keep.tile([P, HALF], F32, name=f"result{h}{m}", align_bytes=64)
-                if m % 2 == 0:
-                    nc.vector.tensor_copy(result[:], acc[:])
-                else:
-                    nc.scalar.copy(result[:], acc[:])
-                nc.sync.dma_start(out[rows, h * HALF : (h + 1) * HALF], result[:])
+
+        def quantize_z(h, cols):
+            nc.vector.quantize_mx(out=z_codes[h][:, cols].bitcast(FP8X4), scales=z_plane[h][:, cols], in_=z_bf[h][:, cols, :].rearrange("p n j -> p (n j)"))
+
+        def product(acc, h, m, cols):
+            places = slice(m % 2 * P, (m % 2 + 1) * P)
+            nc.tensor.matmul_mx(
+                out=acc,
+                lhsT=w1_codes[m // 2][:, places].bitcast(FP8X4),
+                lhsT_scale=w1_plane[m // 2][:, places],
+                rhs=z_codes[h][:, cols].bitcast(FP8X4),
+                rhs_scale=z_plane[h][:, cols],
+                start=True,
+                stop=True,
+            )
+
+        def store(copy, acc, target, name):
+            result = keep.tile([P, HALF], F32, name=name, align_bytes=64)
+            copy(result[:], acc[:])
+            nc.sync.dma_start(target, result[:] if target.ndim == 2 else result[:].rearrange("p (m c) -> p m c", m=2))
+
+        quarters = (slice(0, P), slice(P, HALF))
+        for cols in quarters:
+            quantize_z(0, cols)
+        quantize_w1(1)
+        quantize_z(1, slice(0, HALF))
+        copies = (nc.vector.tensor_copy, nc.scalar.copy)
+        first_rows = out[:HALF, :].rearrange("(m p) c -> p m c", p=P)
+        for q, cols in enumerate(quarters):
+            acc = psum.tile([P, HALF], F32, name="acc")
+            for m in range(2):
+                product(acc[:, quarters[m]], 0, m, cols)
+            store(copies[q], acc, first_rows[:, :, cols], f"early{q}")
+        for h, m in ((0, 2), (0, 3), (1, 0), (1, 1), (1, 2), (1, 3)):
+            acc = psum.tile([P, HALF], F32, name="acc")
+            product(acc[:], h, m, slice(0, HALF))
+            store(copies[m % 2], acc, out[m * P : (m + 1) * P, h * HALF : (h + 1) * HALF], f"result{h}{m}")

@@ -19,7 +19,7 @@ P = 128
 PACK = 4
 HALF = 256
 SHARE = 256
-WA_CUT = (128, 96)
+WA_CUT = (192, 96)
 
 
 def interleave(copy, grouped, raw):
@@ -72,12 +72,10 @@ def tile_picked_mixscat_none_p_kernel(tc, x_words, x_scales, wa, gt, w1, offs, l
             interleave(nc.scalar.copy, wa_bf[h][:, :cut, :], wa_raw[h][:, :, :cut])
             interleave(nc.vector.tensor_copy, wa_bf[h][:, cut:, :], wa_raw[h][:, :, cut:])
             if h == 0:
-                first_plane = keep.tile([P, P], U8, name="first_plane", tag="wa_raw0", align_bytes=64)
-                nc.vector.tensor_copy(first_plane[:], s_dealt[:, 0, :])
+                planes = keep.tile([P, PACK, P], U8, name="planes", tag="wide", align_bytes=64)
+                nc.vector.tensor_copy(planes[:], s_dealt)
             nc.vector.quantize_mx(out=wa_codes[:, cols].bitcast(FP8X4), scales=wa_plane[:, cols], in_=wa_bf[h][:].rearrange("p n j -> p (n j)"))
-        other_planes = keep.tile([P, PACK - 1, P], U8, name="other_planes", tag="wa_bf1", align_bytes=64)
-        nc.vector.tensor_copy(other_planes[:], s_dealt[:, 1:, :])
-        x_planes = [first_plane[:]] + [other_planes[:, t, :] for t in range(PACK - 1)]
+        x_planes = [planes[:, t, :] for t in range(PACK)]
 
         w1_raw = keep.tile([P, PACK, N], F32, name="w1_raw", tag="wide", align_bytes=64)
         nc.sync.dma_start(w1_raw[:], w1.rearrange("(p j) n -> p j n", j=PACK))
@@ -87,7 +85,7 @@ def tile_picked_mixscat_none_p_kernel(tc, x_words, x_scales, wa, gt, w1, offs, l
 
         y = [keep.tile([P, H], F32, name=f"y{t}", tag=f"y{t}", align_bytes=64) for t in range(PACK)]
         for t in range(PACK):
-            pieces = [slice(0, HALF), slice(HALF, H)] if t == 0 else [slice(0, H)]
+            pieces = [slice(0, HALF), slice(HALF, HALF + P), slice(HALF + P, H)] if t == 0 else [slice(0, H)]
             for cols in pieces:
                 acc = psum.tile([P, cols.stop - cols.start], F32, name="acc")
                 nc.tensor.matmul_mx(
@@ -99,7 +97,8 @@ def tile_picked_mixscat_none_p_kernel(tc, x_words, x_scales, wa, gt, w1, offs, l
                     start=True,
                     stop=True,
                 )
-                nc.scalar.copy(y[t][:, cols], acc[:])
+                copy = nc.vector.tensor_copy if cols.start == HALF else nc.scalar.copy
+                copy(y[t][:, cols], acc[:])
 
         z_bf = [keep.tile([P, HALF, PACK], BF16, name=f"z_bf{h}", align_bytes=64) for h in range(2)]
         a = keep.tile([P, PACK, V], F32, name="a", align_bytes=64)
@@ -169,7 +168,7 @@ def tile_picked_mixscat_none_p_kernel(tc, x_words, x_scales, wa, gt, w1, offs, l
             quantize_z(0, cols)
         quantize_w1(1)
         quantize_z(1, slice(0, HALF))
-        copies = (nc.vector.tensor_copy, nc.scalar.copy)
+        copies = (nc.scalar.copy, nc.vector.tensor_copy)
         first_rows = out[:HALF, :].rearrange("(m p) c -> p m c", p=P)
         for q, cols in enumerate(quarters):
             acc = psum.tile([P, HALF], F32, name="acc")

@@ -18,7 +18,6 @@ COPY = mybir.ActivationFunctionType.Copy
 P = 128
 PACK = 4
 HALF = 256
-SHARE = 256
 WA_CUT = (192, 96)
 
 
@@ -116,29 +115,27 @@ def tile_picked_mixscat_none_p_kernel(tc, x_words, x_scales, wa, gt, w1, offs, l
         nc.vector.tensor_tensor(lo[:, 3, :], a[:, 3, :], b[:, 3, :], ALU.min)
         zs = [keep.tile([P, H], F32, name=f"zs{t}", tag=f"zs{t}", align_bytes=64) for t in range(PACK)]
         last = PACK - 1
-        w1_codes = [keep.tile([P, HALF], U32, name=f"w1_codes{h}", tag=("lo", "zs2")[h], align_bytes=64) for h in range(2)]
+        w1_codes = [keep.tile([P, HALF], U32, name=f"w1_codes{h}", tag=("lo", "zs1")[h], align_bytes=64) for h in range(2)]
         w1_plane = [keep.tile([P, HALF], U8, name=f"w1_plane{h}", align_bytes=64) for h in range(2)]
 
         def quantize_w1(h):
             nc.vector.quantize_mx(out=w1_codes[h][:].bitcast(FP8X4), scales=w1_plane[h][:], in_=w1_bf[:, h * HALF : (h + 1) * HALF, :].rearrange("p n j -> p (n j)"))
 
-        for pair in ((0, 1), (2, 3)):
+        for pair in ((2, 0), (1, 3)):
             for t in pair:
                 nc.vector.tensor_copy(zs[t][:].indirect(la_sb[:]), lo[:, t, :])
             for t in pair:
                 nc.vector.tensor_copy(zs[t][:].indirect(lb_sb[:]), hi[:, t, :])
                 scale = gate[:, t : t + 1]
-                if t == last - 1:
-                    nc.scalar.activation(z_bf[0][:, :, t:], zs[t][:, :HALF].unsqueeze(2).to_broadcast([P, HALF, 2]), COPY, scale=scale)
-                elif t == last:
-                    if SHARE < HALF:
-                        nc.scalar.activation(z_bf[0][:, SHARE:, t], zs[t][:, SHARE:HALF], COPY, scale=scale)
-                else:
+                if t < last:
                     nc.scalar.activation(z_bf[0][:, :, t], zs[t][:, :HALF], COPY, scale=scale)
                 nc.scalar.activation(z_bf[1][:, :, t], zs[t][:, HALF:], COPY, scale=scale)
+                if t == last - 1:
+                    last_gate = keep.tile([P, 1], F32, name="last_gate", tag="zs2", align_bytes=64)
+                    nc.scalar.copy(last_gate[:], gate[:, last:])
         quantize_w1(0)
         for c in (0, P):
-            nc.vector.tensor_scalar(z_bf[0][:, c : c + P, last], zs[last][:, c : c + P], gate[:, last:], None, ALU.mult)
+            nc.vector.tensor_scalar(z_bf[0][:, c : c + P, last], zs[last][:, c : c + P], last_gate[:], None, ALU.mult)
 
         z_codes = [keep.tile([P, HALF], U32, name=f"z_codes{h}", align_bytes=64) for h in range(2)]
         z_plane = [keep.tile([P, HALF], U8, name=f"z_plane{h}", align_bytes=64) for h in range(2)]

@@ -18,7 +18,9 @@ COPY = mybir.ActivationFunctionType.Copy
 P = 128
 PACK = 4
 HALF = 256
-WA_CUT = (192, 96)
+LAST = PACK - 1
+BANKS = 8
+SCALAR_COLUMNS = (192, 96)
 
 
 def interleave(copy, grouped, raw):
@@ -28,18 +30,34 @@ def interleave(copy, grouped, raw):
     )
 
 
+def quantize(nc, codes, plane, grouped):
+    nc.vector.quantize_mx(out=codes.bitcast(FP8X4), scales=plane, in_=grouped.rearrange("p n j -> p (n j)"))
+
+
+def multiply(nc, acc, still_codes, still_plane, moving_codes, moving_plane):
+    nc.tensor.matmul_mx(
+        out=acc,
+        lhsT=still_codes.bitcast(FP8X4),
+        lhsT_scale=still_plane,
+        rhs=moving_codes.bitcast(FP8X4),
+        rhs_scale=moving_plane,
+        start=True,
+        stop=True,
+    )
+
+
 def tile_picked_mixscat_none_p_kernel(tc, x_words, x_scales, wa, gt, w1, offs, la, lb, out):
     nc = tc.nc
     with ExitStack() as ctx:
         keep = ctx.enter_context(tc.tile_pool(name="keep", bufs=1))
-        psum = ctx.enter_context(tc.psum_pool(name="psum", bufs=8))
+        psum = ctx.enter_context(tc.psum_pool(name="psum", bufs=BANKS))
 
         offs_sb = keep.tile([P, S // 16], U16, name="offs_sb")
         la_sb = keep.tile([P, V // 16], U16, name="la_sb")
         lb_sb = keep.tile([P, V // 16], U16, name="lb_sb")
-        x_table = keep.tile([P, T], I32, name="x_table", tag="wide", align_bytes=64)
-        s_table = keep.tile([P, T], U8, name="s_table", tag="narrow", align_bytes=64)
-        wa_raw = [keep.tile([P, PACK, HALF], F32, name=f"wa_raw{h}", tag=f"wa_raw{h}", align_bytes=64) for h in range(2)]
+        x_table = keep.tile([P, T], I32, name="x_table", tag="word_table", align_bytes=64)
+        s_table = keep.tile([P, T], U8, name="s_table", tag="scale_table", align_bytes=64)
+        wa_raw = [keep.tile([P, PACK, HALF], F32, name=f"wa_raw{h}", align_bytes=64) for h in range(2)]
 
         s_rows = keep.tile([P, T // 4], I32, name="s_rows", align_bytes=64)
         nc.sync.dma_start(offs_sb[:], offs)
@@ -60,43 +78,42 @@ def tile_picked_mixscat_none_p_kernel(tc, x_words, x_scales, wa, gt, w1, offs, l
         nc.vector.tensor_copy(s_picked[:], s_table[:].indirect(offs_sb[:]))
         x_codes = keep.tile([P, PACK, P], U32, name="x_codes", align_bytes=64)
         nc.vector.tensor_copy(x_codes[:].rearrange("p t m -> p m t"), x_table[:].bitcast(U32).indirect(offs_sb[:]))
-        s_dealt = s_picked[:].rearrange("p (m t) -> p t m", t=PACK)
 
         wa_codes = keep.tile([P, H], U32, name="wa_codes", align_bytes=64)
         wa_plane = keep.tile([P, H], U8, name="wa_plane", align_bytes=64)
-        wa_bf = [keep.tile([P, HALF, PACK], BF16, name=f"wa_bf{h}", tag=f"wa_bf{h}", align_bytes=64) for h in range(2)]
-        for h in range(2):
-            cols = slice(h * HALF, (h + 1) * HALF)
-            cut = WA_CUT[h]
+        wa_bf = [keep.tile([P, HALF, PACK], BF16, name=f"wa_bf{h}", align_bytes=64) for h in range(2)]
+
+        def interleave_wa(h):
+            cut = SCALAR_COLUMNS[h]
             interleave(nc.scalar.copy, wa_bf[h][:, :cut, :], wa_raw[h][:, :, :cut])
             interleave(nc.vector.tensor_copy, wa_bf[h][:, cut:, :], wa_raw[h][:, :, cut:])
-            if h == 0:
-                planes = keep.tile([P, PACK, P], U8, name="planes", tag="wide", align_bytes=64)
-                nc.vector.tensor_copy(planes[:], s_dealt)
-            nc.vector.quantize_mx(out=wa_codes[:, cols].bitcast(FP8X4), scales=wa_plane[:, cols], in_=wa_bf[h][:].rearrange("p n j -> p (n j)"))
-        x_planes = [planes[:, t, :] for t in range(PACK)]
 
-        w1_raw = keep.tile([P, PACK, N], F32, name="w1_raw", tag="wide", align_bytes=64)
+        def quantize_wa(h):
+            cols = slice(h * HALF, (h + 1) * HALF)
+            quantize(nc, wa_codes[:, cols], wa_plane[:, cols], wa_bf[h][:])
+
+        interleave_wa(0)
+        x_planes = keep.tile([P, PACK, P], U8, name="x_planes", tag="word_table", align_bytes=64)
+        nc.vector.tensor_copy(x_planes[:], s_picked[:].rearrange("p (m t) -> p t m", t=PACK))
+        quantize_wa(0)
+        interleave_wa(1)
+        quantize_wa(1)
+
+        w1_raw = keep.tile([P, PACK, N], F32, name="w1_raw", tag="word_table", align_bytes=64)
         nc.sync.dma_start(w1_raw[:], w1.rearrange("(p j) n -> p j n", j=PACK))
-        gate = keep.tile([P, PACK], F32, name="gate", tag="narrow", align_bytes=64)
+        gate = keep.tile([P, PACK], F32, name="gate", tag="scale_table", align_bytes=64)
         nc.sync.dma_start(gate[:], gt.rearrange("(p t) o -> p (t o)", t=PACK))
 
-
         y = [keep.tile([P, H], F32, name=f"y{t}", tag=f"y{t}", align_bytes=64) for t in range(PACK)]
+        first_tile_pieces = (
+            (slice(0, HALF), nc.scalar.copy),
+            (slice(HALF, HALF + P), nc.vector.tensor_copy),
+            (slice(HALF + P, H), nc.scalar.copy),
+        )
         for t in range(PACK):
-            pieces = [slice(0, HALF), slice(HALF, HALF + P), slice(HALF + P, H)] if t == 0 else [slice(0, H)]
-            for cols in pieces:
+            for cols, copy in first_tile_pieces if t == 0 else [(slice(0, H), nc.scalar.copy)]:
                 acc = psum.tile([P, cols.stop - cols.start], F32, name="acc")
-                nc.tensor.matmul_mx(
-                    out=acc[:],
-                    lhsT=x_codes[:, t, :].bitcast(FP8X4),
-                    lhsT_scale=x_planes[t],
-                    rhs=wa_codes[:, cols].bitcast(FP8X4),
-                    rhs_scale=wa_plane[:, cols],
-                    start=True,
-                    stop=True,
-                )
-                copy = nc.vector.tensor_copy if cols.start == HALF else nc.scalar.copy
+                multiply(nc, acc[:], x_codes[:, t, :], x_planes[:, t, :], wa_codes[:, cols], wa_plane[:, cols])
                 copy(y[t][:, cols], acc[:])
 
         z_bf = [keep.tile([P, HALF, PACK], BF16, name=f"z_bf{h}", align_bytes=64) for h in range(2)]
@@ -105,74 +122,57 @@ def tile_picked_mixscat_none_p_kernel(tc, x_words, x_scales, wa, gt, w1, offs, l
         for t in range(PACK):
             nc.vector.tensor_copy(a[:, t, :], y[t][:].indirect(la_sb[:]))
             nc.vector.tensor_copy(b[:, t, :], y[t][:].indirect(lb_sb[:]))
-        w1_bf = keep.tile([P, N, PACK], BF16, name="w1_bf", tag="y3", align_bytes=64)
+        w1_bf = keep.tile([P, N, PACK], BF16, name="w1_bf", tag=f"y{LAST}", align_bytes=64)
         interleave(nc.scalar.copy, w1_bf[:], w1_raw[:])
 
-        lo = keep.tile([P, PACK, V], F32, name="lo", tag="lo", align_bytes=64)
-        hi = keep.tile([P, PACK, V], F32, name="hi", align_bytes=64)
-        nc.vector.tensor_tensor(lo[:, :3, :], a[:, :3, :], b[:, :3, :], ALU.min)
-        nc.vector.tensor_tensor(hi[:], a[:], b[:], ALU.max)
-        nc.vector.tensor_tensor(lo[:, 3, :], a[:, 3, :], b[:, 3, :], ALU.min)
+        mn = keep.tile([P, PACK, V], F32, name="mn", tag="mn", align_bytes=64)
+        mx = keep.tile([P, PACK, V], F32, name="mx", align_bytes=64)
+        nc.vector.tensor_tensor(mn[:, :LAST, :], a[:, :LAST, :], b[:, :LAST, :], ALU.min)
+        nc.vector.tensor_tensor(mx[:], a[:], b[:], ALU.max)
+        nc.vector.tensor_tensor(mn[:, LAST, :], a[:, LAST, :], b[:, LAST, :], ALU.min)
+
         zs = [keep.tile([P, H], F32, name=f"zs{t}", tag=f"zs{t}", align_bytes=64) for t in range(PACK)]
-        last = PACK - 1
-        w1_codes = [keep.tile([P, HALF], U32, name=f"w1_codes{h}", tag=("lo", "zs1")[h], align_bytes=64) for h in range(2)]
+        scatter_pairs = ((LAST - 1, 0), (1, LAST))
+        w1_tags = ("mn", f"zs{scatter_pairs[1][0]}")
+        w1_codes = [keep.tile([P, HALF], U32, name=f"w1_codes{h}", tag=w1_tags[h], align_bytes=64) for h in range(2)]
         w1_plane = [keep.tile([P, HALF], U8, name=f"w1_plane{h}", align_bytes=64) for h in range(2)]
 
         def quantize_w1(h):
-            nc.vector.quantize_mx(out=w1_codes[h][:].bitcast(FP8X4), scales=w1_plane[h][:], in_=w1_bf[:, h * HALF : (h + 1) * HALF, :].rearrange("p n j -> p (n j)"))
+            quantize(nc, w1_codes[h][:], w1_plane[h][:], w1_bf[:, h * HALF : (h + 1) * HALF, :])
 
-        for pair in ((2, 0), (1, 3)):
+        for pair in scatter_pairs:
             for t in pair:
-                nc.vector.tensor_copy(zs[t][:].indirect(la_sb[:]), lo[:, t, :])
+                nc.vector.tensor_copy(zs[t][:].indirect(la_sb[:]), mn[:, t, :])
             for t in pair:
-                nc.vector.tensor_copy(zs[t][:].indirect(lb_sb[:]), hi[:, t, :])
-                scale = gate[:, t : t + 1]
-                if t < last:
-                    nc.scalar.activation(z_bf[0][:, :, t], zs[t][:, :HALF], COPY, scale=scale)
-                nc.scalar.activation(z_bf[1][:, :, t], zs[t][:, HALF:], COPY, scale=scale)
-                if t == last - 1:
-                    last_gate = keep.tile([P, 1], F32, name="last_gate", tag="zs2", align_bytes=64)
-                    nc.scalar.copy(last_gate[:], gate[:, last:])
-        quantize_w1(0)
-        for c in (0, P):
-            nc.vector.tensor_scalar(z_bf[0][:, c : c + P, last], zs[last][:, c : c + P], last_gate[:], None, ALU.mult)
-
-        z_codes = [keep.tile([P, HALF], U32, name=f"z_codes{h}", align_bytes=64) for h in range(2)]
-        z_plane = [keep.tile([P, HALF], U8, name=f"z_plane{h}", align_bytes=64) for h in range(2)]
-
-        def quantize_z(h, cols):
-            nc.vector.quantize_mx(out=z_codes[h][:, cols].bitcast(FP8X4), scales=z_plane[h][:, cols], in_=z_bf[h][:, cols, :].rearrange("p n j -> p (n j)"))
-
-        def product(acc, h, m, cols):
-            places = slice(m % 2 * P, (m % 2 + 1) * P)
-            nc.tensor.matmul_mx(
-                out=acc,
-                lhsT=w1_codes[m // 2][:, places].bitcast(FP8X4),
-                lhsT_scale=w1_plane[m // 2][:, places],
-                rhs=z_codes[h][:, cols].bitcast(FP8X4),
-                rhs_scale=z_plane[h][:, cols],
-                start=True,
-                stop=True,
-            )
-
-        def store(copy, acc, target, name):
-            result = keep.tile([P, HALF], F32, name=name, align_bytes=64)
-            copy(result[:], acc[:])
-            nc.sync.dma_start(target, result[:] if target.ndim == 2 else result[:].rearrange("p (m c) -> p m c", m=2))
+                nc.vector.tensor_copy(zs[t][:].indirect(lb_sb[:]), mx[:, t, :])
+                for h in range(2) if t < LAST else [1]:
+                    nc.scalar.activation(z_bf[h][:, :, t], zs[t][:, h * HALF : (h + 1) * HALF], COPY, scale=gate[:, t : t + 1])
+                if t == LAST - 1:
+                    last_gate = keep.tile([P, 1], F32, name="last_gate", tag=f"zs{t}", align_bytes=64)
+                    nc.scalar.copy(last_gate[:], gate[:, LAST:])
 
         quarters = (slice(0, P), slice(P, HALF))
+        whole_half = slice(0, HALF)
+        quantize_w1(0)
         for cols in quarters:
-            quantize_z(0, cols)
+            nc.vector.tensor_scalar(z_bf[0][:, cols, LAST], zs[LAST][:, cols], last_gate[:], None, ALU.mult)
+        z_codes = [keep.tile([P, HALF], U32, name=f"z_codes{h}", align_bytes=64) for h in range(2)]
+        z_plane = [keep.tile([P, HALF], U8, name=f"z_plane{h}", align_bytes=64) for h in range(2)]
+        for cols in quarters:
+            quantize(nc, z_codes[0][:, cols], z_plane[0][:, cols], z_bf[0][:, cols, :])
         quantize_w1(1)
-        quantize_z(1, slice(0, HALF))
+        quantize(nc, z_codes[1][:], z_plane[1][:], z_bf[1][:])
+
+        def mix(acc, h, m, cols):
+            places = slice(m % 2 * P, (m % 2 + 1) * P)
+            multiply(nc, acc, w1_codes[m // 2][:, places], w1_plane[m // 2][:, places], z_codes[h][:, cols], z_plane[h][:, cols])
+
         copies = (nc.scalar.copy, nc.vector.tensor_copy)
-        first_rows = out[:HALF, :].rearrange("(m p) c -> p m c", p=P)
-        for q, cols in enumerate(quarters):
-            acc = psum.tile([P, HALF], F32, name="acc")
-            for m in range(2):
-                product(acc[:, quarters[m]], 0, m, cols)
-            store(copies[q], acc, first_rows[:, :, cols], f"early{q}")
-        for h, m in ((0, 2), (0, 3), (1, 0), (1, 1), (1, 2), (1, 3)):
-            acc = psum.tile([P, HALF], F32, name="acc")
-            product(acc[:], h, m, slice(0, HALF))
-            store(copies[m % 2], acc, out[m * P : (m + 1) * P, h * HALF : (h + 1) * HALF], f"result{h}{m}")
+        for h in range(2):
+            for m in range(N // P):
+                result = keep.tile([P, HALF], F32, name=f"result{h}{m}", align_bytes=64)
+                for cols in quarters if h == m == 0 else [whole_half]:
+                    acc = psum.tile([P, cols.stop - cols.start], F32, name="acc")
+                    mix(acc[:], h, m, cols)
+                    copies[m % 2](result[:, cols], acc[:])
+                nc.sync.dma_start(out[m * P : (m + 1) * P, h * HALF : (h + 1) * HALF], result[:])

@@ -20,7 +20,7 @@ PACK = 4
 HALF = 256
 LAST = PACK - 1
 BANKS = 8
-SCALAR_COLUMNS = (192, 96)
+SCALAR_COLUMNS = (160, 96)
 
 
 def interleave(copy, grouped, raw):
@@ -57,13 +57,11 @@ def tile_picked_mixscat_none_p_kernel(tc, x_words, x_scales, wa, gt, w1, offs, l
         lb_sb = keep.tile([P, V // 16], U16, name="lb_sb")
         x_table = keep.tile([P, T], I32, name="x_table", tag="word_table", align_bytes=64)
         s_table = keep.tile([P, T], U8, name="s_table", tag="scale_table", align_bytes=64)
-        wa_raw = [keep.tile([P, PACK, HALF], F32, name=f"wa_raw{h}", align_bytes=64) for h in range(2)]
+        wa_raw = [keep.tile([P, PACK, HALF], F32, name=f"wa_raw{h}", tag=f"wa_raw{h}", align_bytes=64) for h in range(2)]
 
         s_rows = keep.tile([P, T // 4], I32, name="s_rows", align_bytes=64)
         nc.sync.dma_start(offs_sb[:], offs)
-        for q in range(4):
-            queue = nc.sync if q < 2 else nc.scalar
-            queue.dma_start(s_rows[32 * q : 32 * q + 4, :], x_scales[0, 4 * q : 4 * q + 4, :].bitcast(I32))
+        nc.scalar.dma_start(s_rows[:16, :], x_scales[0].bitcast(I32))
         nc.sync.dma_start(x_table[:], x_words[0].rearrange("p n r -> p (n r)").bitcast(I32))
         wa_rows = wa.rearrange("(p j) n -> p j n", j=PACK)
         for h in range(2):
@@ -72,10 +70,14 @@ def tile_picked_mixscat_none_p_kernel(tc, x_words, x_scales, wa, gt, w1, offs, l
         nc.sync.dma_start(lb_sb[:], lb)
 
         nc.vector.memset(s_table[:].bitcast(I32), 0)
-        for q in range(4):
-            nc.vector.tensor_copy(s_table[32 * q : 32 * q + 4, :].bitcast(I32), s_rows[32 * q : 32 * q + 4, :])
+        nc.vector.tensor_copy(s_table[:16, :].bitcast(I32), s_rows[:16, :])
         s_picked = keep.tile([P, S], U8, name="s_picked", align_bytes=64)
         nc.vector.tensor_copy(s_picked[:], s_table[:].indirect(offs_sb[:]))
+        x_planes = keep.tile([P, PACK, P], U8, name="x_planes", align_bytes=64)
+        nc.vector.tensor_copy(x_planes[:], s_picked[:].rearrange("p (m t) -> p t m", t=PACK))
+        plane_words = x_planes[:].rearrange("p t m -> p (t m)").bitcast(I32)
+        for q in range(1, 4):
+            nc.sync.dma_start(plane_words[32 * q : 32 * q + 4, :], plane_words[4 * q : 4 * q + 4, :])
         x_codes = keep.tile([P, PACK, P], U32, name="x_codes", align_bytes=64)
         nc.vector.tensor_copy(x_codes[:].rearrange("p t m -> p m t"), x_table[:].bitcast(U32).indirect(offs_sb[:]))
 
@@ -93,15 +95,13 @@ def tile_picked_mixscat_none_p_kernel(tc, x_words, x_scales, wa, gt, w1, offs, l
             quantize(nc, wa_codes[:, cols], wa_plane[:, cols], wa_bf[h][:])
 
         interleave_wa(0)
-        x_planes = keep.tile([P, PACK, P], U8, name="x_planes", tag="word_table", align_bytes=64)
-        nc.vector.tensor_copy(x_planes[:], s_picked[:].rearrange("p (m t) -> p t m", t=PACK))
         quantize_wa(0)
         interleave_wa(1)
         quantize_wa(1)
 
-        w1_raw = keep.tile([P, PACK, N], F32, name="w1_raw", tag="word_table", align_bytes=64)
+        w1_raw = keep.tile([P, PACK, N], F32, name="w1_raw", tag="wa_raw1", align_bytes=64)
         nc.sync.dma_start(w1_raw[:], w1.rearrange("(p j) n -> p j n", j=PACK))
-        gate = keep.tile([P, PACK], F32, name="gate", tag="scale_table", align_bytes=64)
+        gate = keep.tile([P, PACK], F32, name="gate", tag="word_table", align_bytes=64)
         nc.sync.dma_start(gate[:], gt.rearrange("(p t) o -> p (t o)", t=PACK))
 
         y = [keep.tile([P, H], F32, name=f"y{t}", tag=f"y{t}", align_bytes=64) for t in range(PACK)]

@@ -20,7 +20,7 @@ PACK = 4
 HALF = 256
 LAST = PACK - 1
 BANKS = 8
-SCALAR_COLUMNS = (160, 96)
+SCALAR_COLUMNS = ((256, 64), (80, 80))
 
 
 def interleave(copy, grouped, raw):
@@ -57,7 +57,7 @@ def tile_picked_mixscat_none_p_kernel(tc, x_words, x_scales, wa, gt, w1, offs, l
         lb_sb = keep.tile([P, V // 16], U16, name="lb_sb")
         x_table = keep.tile([P, T], I32, name="x_table", tag="word_table", align_bytes=64)
         s_table = keep.tile([P, T], U8, name="s_table", tag="scale_table", align_bytes=64)
-        wa_raw = [keep.tile([P, PACK, HALF], F32, name=f"wa_raw{h}", tag=f"wa_raw{h}", align_bytes=64) for h in range(2)]
+        wa_raw = [keep.tile([P, 2, H], F32, name=f"wa_raw{h}", tag=f"wa_raw{h}", align_bytes=64) for h in range(2)]
 
         s_rows = keep.tile([P, T // 4], I32, name="s_rows", align_bytes=64)
         nc.sync.dma_start(offs_sb[:], offs)
@@ -65,7 +65,7 @@ def tile_picked_mixscat_none_p_kernel(tc, x_words, x_scales, wa, gt, w1, offs, l
         nc.sync.dma_start(x_table[:], x_words[0].rearrange("p n r -> p (n r)").bitcast(I32))
         wa_rows = wa.rearrange("(p j) n -> p j n", j=PACK)
         for h in range(2):
-            nc.sync.dma_start(wa_raw[h][:], wa_rows[:, :, h * HALF : (h + 1) * HALF])
+            nc.sync.dma_start(wa_raw[h][:], wa_rows[:, 2 * h : 2 * h + 2, :])
         nc.sync.dma_start(la_sb[:], la)
         nc.sync.dma_start(lb_sb[:], lb)
 
@@ -85,18 +85,22 @@ def tile_picked_mixscat_none_p_kernel(tc, x_words, x_scales, wa, gt, w1, offs, l
         wa_plane = keep.tile([P, H], U8, name="wa_plane", align_bytes=64)
         wa_bf = [keep.tile([P, HALF, PACK], BF16, name=f"wa_bf{h}", align_bytes=64) for h in range(2)]
 
-        def interleave_wa(h):
-            cut = SCALAR_COLUMNS[h]
-            interleave(nc.scalar.copy, wa_bf[h][:, :cut, :], wa_raw[h][:, :, :cut])
-            interleave(nc.vector.tensor_copy, wa_bf[h][:, cut:, :], wa_raw[h][:, :, cut:])
+        def interleave_wa(pair):
+            places = slice(2 * pair, 2 * pair + 2)
+            for h in range(2):
+                cut = SCALAR_COLUMNS[pair][h]
+                raw = wa_raw[pair][:, :, h * HALF : (h + 1) * HALF]
+                interleave(nc.scalar.copy, wa_bf[h][:, :cut, places], raw[:, :, :cut])
+                if cut < HALF:
+                    interleave(nc.vector.tensor_copy, wa_bf[h][:, cut:, places], raw[:, :, cut:])
 
         def quantize_wa(h):
             cols = slice(h * HALF, (h + 1) * HALF)
             quantize(nc, wa_codes[:, cols], wa_plane[:, cols], wa_bf[h][:])
 
         interleave_wa(0)
-        quantize_wa(0)
         interleave_wa(1)
+        quantize_wa(0)
         quantize_wa(1)
 
         w1_raw = keep.tile([P, PACK, N], F32, name="w1_raw", tag="wa_raw1", align_bytes=64)

@@ -14,6 +14,7 @@ U8 = mybir.dt.uint8
 FP8X4 = mybir.dt.float8_e4m3fn_x4
 ALU = mybir.AluOpType
 COPY = mybir.ActivationFunctionType.Copy
+SIGN = mybir.ActivationFunctionType.Sign
 
 P = 128
 PACK = 4
@@ -114,46 +115,62 @@ def tile_picked_mixscat_none_p_kernel(tc, x_words, x_scales, wa, gt, w1, offs, l
             (slice(HALF, HALF + P), nc.vector.tensor_copy),
             (slice(HALF + P, H), nc.scalar.copy),
         )
-        for t in range(PACK):
+        for t in (0, 1, LAST, LAST - 1):
             for cols, copy in first_tile_pieces if t == 0 else [(slice(0, H), nc.scalar.copy)]:
                 acc = psum.tile([P, cols.stop - cols.start], F32, name="acc")
                 multiply(nc, acc[:], x_codes[:, t, :], x_planes[:, t, :], wa_codes[:, cols], wa_plane[:, cols])
                 copy(y[t][:, cols], acc[:])
 
-        z_bf = [keep.tile([P, HALF, PACK], BF16, name=f"z_bf{h}", align_bytes=64) for h in range(2)]
-        a = keep.tile([P, PACK, V], F32, name="a", align_bytes=64)
-        b = keep.tile([P, PACK, V], F32, name="b", align_bytes=64)
-        for t in range(PACK):
-            nc.vector.tensor_copy(a[:, t, :], y[t][:].indirect(la_sb[:]))
-            nc.vector.tensor_copy(b[:, t, :], y[t][:].indirect(lb_sb[:]))
-        w1_bf = keep.tile([P, N, PACK], BF16, name="w1_bf", tag=f"y{LAST}", align_bytes=64)
-        interleave(nc.scalar.copy, w1_bf[:], w1_raw[:])
-
-        mn = keep.tile([P, PACK, V], F32, name="mn", tag="mn", align_bytes=64)
+        order = (0, 1, LAST, LAST - 1)
+        ab = keep.tile([P, PACK, 2, V], F32, name="ab", align_bytes=64)
         mx = keep.tile([P, PACK, V], F32, name="mx", align_bytes=64)
-        nc.vector.tensor_tensor(mn[:, :LAST, :], a[:, :LAST, :], b[:, :LAST, :], ALU.min)
-        nc.vector.tensor_tensor(mx[:], a[:], b[:], ALU.max)
-        nc.vector.tensor_tensor(mn[:, LAST, :], a[:, LAST, :], b[:, LAST, :], ALU.min)
+        mn = [keep.tile([P, V], F32, name=f"mn{i}", tag=f"mn{i}", align_bytes=64) for i in range(PACK)]
+        for i, t in enumerate(order):
+            nc.vector.tensor_copy(ab[:, i, 0, :], y[t][:].indirect(la_sb[:]))
+            nc.vector.tensor_copy(ab[:, i, 1, :], y[t][:].indirect(lb_sb[:]))
+        w1_bf = keep.tile([P, N, PACK], BF16, name="w1_bf", tag=f"y{order[-1]}", align_bytes=64)
+        interleave(nc.scalar.copy, w1_bf[:], w1_raw[:])
+        nc.vector.tensor_tensor(mx[:], ab[:, :, 0, :], ab[:, :, 1, :], ALU.max)
+        nc.vector.tensor_tensor(mn[LAST][:], ab[:, LAST, 0, :], ab[:, LAST, 1, :], ALU.min)
+        below = keep.tile([P, LAST, V], F32, name="below", tag="below", align_bytes=64)
+        weights = keep.tile([P, LAST, 2, V], F32, name="weights", align_bytes=64)
+        chosen = keep.tile([P, LAST, 2, V], F32, name="chosen", align_bytes=64)
+        for part in (slice(0, 1), slice(1, LAST)):
+            nc.gpsimd.tensor_tensor(below[:, part, :], ab[:, part, 0, :], mx[:, part, :], ALU.subtract)
+            nc.scalar.activation(weights[:, part, 0, :], below[:, part, :], SIGN)
+            nc.scalar.activation(weights[:, part, 1, :], weights[:, part, 0, :], COPY, bias=1.0)
+        for i in range(LAST):
+            nc.gpsimd.tensor_tensor(chosen[:, i, :, :], ab[:, i, :, :], weights[:, i, :, :], ALU.mult)
+            nc.gpsimd.tensor_tensor(mn[i][:], chosen[:, i, 1, :], chosen[:, i, 0, :], ALU.subtract)
 
+        z_both = keep.tile([P, H, PACK], BF16, name="z_both", tag="below", align_bytes=64)
+        z_bf = [z_both[:, h * HALF : (h + 1) * HALF, :] for h in range(2)]
         zs = [keep.tile([P, H], F32, name=f"zs{t}", tag=f"zs{t}", align_bytes=64) for t in range(PACK)]
-        scatter_pairs = ((LAST - 1, 0), (1, LAST))
-        w1_tags = ("mn", f"zs{scatter_pairs[1][0]}")
+        w1_tags = ("mn0", "zs1")
         w1_codes = [keep.tile([P, HALF], U32, name=f"w1_codes{h}", tag=w1_tags[h], align_bytes=64) for h in range(2)]
         w1_plane = [keep.tile([P, HALF], U8, name=f"w1_plane{h}", align_bytes=64) for h in range(2)]
 
         def quantize_w1(h):
             quantize(nc, w1_codes[h][:], w1_plane[h][:], w1_bf[:, h * HALF : (h + 1) * HALF, :])
 
-        for pair in scatter_pairs:
-            for t in pair:
-                nc.vector.tensor_copy(zs[t][:].indirect(la_sb[:]), mn[:, t, :])
-            for t in pair:
-                nc.vector.tensor_copy(zs[t][:].indirect(lb_sb[:]), mx[:, t, :])
-                for h in range(2) if t < LAST else [1]:
-                    nc.scalar.activation(z_bf[h][:, :, t], zs[t][:, h * HALF : (h + 1) * HALF], COPY, scale=gate[:, t : t + 1])
-                if t == LAST - 1:
-                    last_gate = keep.tile([P, 1], F32, name="last_gate", tag=f"zs{t}", align_bytes=64)
-                    nc.scalar.copy(last_gate[:], gate[:, LAST:])
+        def scatter_mx(i):
+            nc.vector.tensor_copy(zs[order[i]][:].indirect(lb_sb[:]), mx[:, i, :])
+
+        def scatter_mn(i):
+            t = order[i]
+            nc.vector.tensor_copy(zs[t][:].indirect(la_sb[:]), mn[i][:])
+            for h in range(2) if t < LAST else [1]:
+                nc.scalar.activation(z_bf[h][:, :, t], zs[t][:, h * HALF : (h + 1) * HALF], COPY, scale=gate[:, t : t + 1])
+
+        scatter_mx(LAST)
+        scatter_mx(0)
+        scatter_mn(LAST)
+        last_gate = keep.tile([P, 1], F32, name="last_gate", tag=f"zs{LAST - 1}", align_bytes=64)
+        nc.scalar.copy(last_gate[:], gate[:, LAST:])
+        for i in range(1, LAST):
+            scatter_mx(i)
+        for i in range(LAST):
+            scatter_mn(i)
 
         quarters = (slice(0, P), slice(P, HALF))
         whole_half = slice(0, HALF)
@@ -165,7 +182,7 @@ def tile_picked_mixscat_none_p_kernel(tc, x_words, x_scales, wa, gt, w1, offs, l
         for cols in quarters:
             quantize(nc, z_codes[0][:, cols], z_plane[0][:, cols], z_bf[0][:, cols, :])
         quantize_w1(1)
-        quantize(nc, z_codes[1][:], z_plane[1][:], z_bf[1][:])
+        quantize(nc, z_codes[1][:], z_plane[1][:], z_bf[1])
 
         def mix(acc, h, m, cols):
             places = slice(m % 2 * P, (m % 2 + 1) * P)

@@ -21,6 +21,7 @@ PACK = 4
 HALF = 256
 LAST = PACK - 1
 BANKS = 8
+SCALE_ROWS = K // 32
 SCALAR_COLUMNS = ((256, 64), (80, 80))
 
 
@@ -56,22 +57,22 @@ def tile_picked_mixscat_none_p_kernel(tc, x_words, x_scales, wa, gt, w1, offs, l
         offs_sb = keep.tile([P, S // 16], U16, name="offs_sb")
         la_sb = keep.tile([P, V // 16], U16, name="la_sb")
         lb_sb = keep.tile([P, V // 16], U16, name="lb_sb")
-        x_table = keep.tile([P, T], I32, name="x_table", tag="word_table", align_bytes=64)
-        s_table = keep.tile([P, T], U8, name="s_table", tag="scale_table", align_bytes=64)
-        wa_raw = [keep.tile([P, 2, H], F32, name=f"wa_raw{h}", tag=f"wa_raw{h}", align_bytes=64) for h in range(2)]
+        x_table = keep.tile([P, T], I32, name="x_table", tag="x_table", align_bytes=64)
+        s_table = keep.tile([P, T], U8, name="s_table", align_bytes=64)
+        wa_raw = [keep.tile([P, 2, H], F32, name=f"wa_raw{i}", tag=f"wa_raw{i}", align_bytes=64) for i in range(2)]
 
         s_rows = keep.tile([P, T // 4], I32, name="s_rows", align_bytes=64)
         nc.sync.dma_start(offs_sb[:], offs)
-        nc.scalar.dma_start(s_rows[:16, :], x_scales[0].bitcast(I32))
+        nc.scalar.dma_start(s_rows[:SCALE_ROWS, :], x_scales[0].bitcast(I32))
         nc.sync.dma_start(x_table[:], x_words[0].rearrange("p n r -> p (n r)").bitcast(I32))
         wa_rows = wa.rearrange("(p j) n -> p j n", j=PACK)
-        for h in range(2):
-            nc.sync.dma_start(wa_raw[h][:], wa_rows[:, 2 * h : 2 * h + 2, :])
+        for i in range(2):
+            nc.sync.dma_start(wa_raw[i][:], wa_rows[:, 2 * i : 2 * i + 2, :])
         nc.sync.dma_start(la_sb[:], la)
         nc.sync.dma_start(lb_sb[:], lb)
 
         nc.vector.memset(s_table[:].bitcast(I32), 0)
-        nc.vector.tensor_copy(s_table[:16, :].bitcast(I32), s_rows[:16, :])
+        nc.vector.tensor_copy(s_table[:SCALE_ROWS, :].bitcast(I32), s_rows[:SCALE_ROWS, :])
         s_picked = keep.tile([P, S], U8, name="s_picked", align_bytes=64)
         nc.vector.tensor_copy(s_picked[:], s_table[:].indirect(offs_sb[:]))
         x_planes = keep.tile([P, PACK, P], U8, name="x_planes", align_bytes=64)
@@ -85,29 +86,27 @@ def tile_picked_mixscat_none_p_kernel(tc, x_words, x_scales, wa, gt, w1, offs, l
         wa_codes = keep.tile([P, H], U32, name="wa_codes", align_bytes=64)
         wa_plane = keep.tile([P, H], U8, name="wa_plane", align_bytes=64)
         wa_bf = [keep.tile([P, HALF, PACK], BF16, name=f"wa_bf{h}", align_bytes=64) for h in range(2)]
-
-        def interleave_wa(pair):
-            places = slice(2 * pair, 2 * pair + 2)
+        for i in range(2):
+            places = slice(2 * i, 2 * i + 2)
             for h in range(2):
-                cut = SCALAR_COLUMNS[pair][h]
-                raw = wa_raw[pair][:, :, h * HALF : (h + 1) * HALF]
+                cut = SCALAR_COLUMNS[i][h]
+                raw = wa_raw[i][:, :, h * HALF : (h + 1) * HALF]
                 interleave(nc.scalar.copy, wa_bf[h][:, :cut, places], raw[:, :, :cut])
                 if cut < HALF:
                     interleave(nc.vector.tensor_copy, wa_bf[h][:, cut:, places], raw[:, :, cut:])
-
-        def quantize_wa(h):
+        for h in range(2):
             cols = slice(h * HALF, (h + 1) * HALF)
             quantize(nc, wa_codes[:, cols], wa_plane[:, cols], wa_bf[h][:])
 
-        interleave_wa(0)
-        interleave_wa(1)
-        quantize_wa(0)
-        quantize_wa(1)
-
         w1_raw = keep.tile([P, PACK, N], F32, name="w1_raw", tag="wa_raw1", align_bytes=64)
         nc.sync.dma_start(w1_raw[:], w1.rearrange("(p j) n -> p j n", j=PACK))
-        gate = keep.tile([P, PACK], F32, name="gate", tag="word_table", align_bytes=64)
+        gate = keep.tile([P, PACK], F32, name="gate", tag="x_table", align_bytes=64)
         nc.sync.dma_start(gate[:], gt.rearrange("(p t) o -> p (t o)", t=PACK))
+
+        early = (0, 1)
+        own = LAST - 1
+        gather_order = (*early, LAST, own)
+        helped = (*early, LAST)
 
         y = [keep.tile([P, H], F32, name=f"y{t}", tag=f"y{t}", align_bytes=64) for t in range(PACK)]
         first_tile_pieces = (
@@ -115,62 +114,75 @@ def tile_picked_mixscat_none_p_kernel(tc, x_words, x_scales, wa, gt, w1, offs, l
             (slice(HALF, HALF + P), nc.vector.tensor_copy),
             (slice(HALF + P, H), nc.scalar.copy),
         )
-        for t in (0, 1, LAST, LAST - 1):
-            for cols, copy in first_tile_pieces if t == 0 else [(slice(0, H), nc.scalar.copy)]:
+        for t in gather_order:
+            for cols, copy in first_tile_pieces if t == gather_order[0] else [(slice(0, H), nc.scalar.copy)]:
                 acc = psum.tile([P, cols.stop - cols.start], F32, name="acc")
                 multiply(nc, acc[:], x_codes[:, t, :], x_planes[:, t, :], wa_codes[:, cols], wa_plane[:, cols])
                 copy(y[t][:, cols], acc[:])
 
-        order = (0, 1, LAST, LAST - 1)
-        ab = keep.tile([P, PACK, 2, V], F32, name="ab", align_bytes=64)
-        mx = keep.tile([P, PACK, V], F32, name="mx", align_bytes=64)
-        mn = [keep.tile([P, V], F32, name=f"mn{i}", tag=f"mn{i}", align_bytes=64) for i in range(PACK)]
-        for i, t in enumerate(order):
-            nc.vector.tensor_copy(ab[:, i, 0, :], y[t][:].indirect(la_sb[:]))
-            nc.vector.tensor_copy(ab[:, i, 1, :], y[t][:].indirect(lb_sb[:]))
-        w1_bf = keep.tile([P, N, PACK], BF16, name="w1_bf", tag=f"y{order[-1]}", align_bytes=64)
-        interleave(nc.scalar.copy, w1_bf[:], w1_raw[:])
-        nc.vector.tensor_tensor(mx[:], ab[:, :, 0, :], ab[:, :, 1, :], ALU.max)
-        nc.vector.tensor_tensor(mn[LAST][:], ab[:, LAST, 0, :], ab[:, LAST, 1, :], ALU.min)
-        below = keep.tile([P, LAST, V], F32, name="below", tag="below", align_bytes=64)
-        weights = keep.tile([P, LAST, 2, V], F32, name="weights", align_bytes=64)
-        chosen = keep.tile([P, LAST, 2, V], F32, name="chosen", align_bytes=64)
-        for part in (slice(0, 1), slice(1, LAST)):
-            nc.gpsimd.tensor_tensor(below[:, part, :], ab[:, part, 0, :], mx[:, part, :], ALU.subtract)
-            nc.scalar.activation(weights[:, part, 0, :], below[:, part, :], SIGN)
-            nc.scalar.activation(weights[:, part, 1, :], weights[:, part, 0, :], COPY, bias=1.0)
-        for i in range(LAST):
-            nc.gpsimd.tensor_tensor(chosen[:, i, :, :], ab[:, i, :, :], weights[:, i, :, :], ALU.mult)
-            nc.gpsimd.tensor_tensor(mn[i][:], chosen[:, i, 1, :], chosen[:, i, 0, :], ALU.subtract)
+        ab = {t: keep.tile([P, 2, V], F32, name=f"ab{t}", tag=f"ab{t}", align_bytes=64) for t in gather_order}
+        for t in gather_order:
+            nc.vector.tensor_copy(ab[t][:, 0, :], y[t][:].indirect(la_sb[:]))
+            nc.vector.tensor_copy(ab[t][:, 1, :], y[t][:].indirect(lb_sb[:]))
 
-        z_both = keep.tile([P, H, PACK], BF16, name="z_both", tag="below", align_bytes=64)
+        diff = keep.tile([P, len(helped), V], F32, name="diff", tag="diff", align_bytes=64)
+        signs = keep.tile([P, len(helped), V], F32, name="signs", tag="signs", align_bytes=64)
+        weights = keep.tile([P, len(helped), 2, V], F32, name="weights", align_bytes=64)
+        for n, t in enumerate(helped):
+            nc.gpsimd.tensor_tensor(diff[:, n, :], ab[t][:, 0, :], ab[t][:, 1, :], ALU.subtract)
+            nc.scalar.activation(signs[:, n, :], diff[:, n, :], SIGN)
+            nc.scalar.activation(weights[:, n, 0, :], signs[:, n, :], COPY, scale=-0.5, bias=0.5)
+            nc.scalar.activation(weights[:, n, 1, :], signs[:, n, :], COPY, scale=0.5, bias=0.5)
+        w1_bf = keep.tile([P, N, PACK], BF16, name="w1_bf", tag="signs", align_bytes=64)
+        interleave(nc.scalar.copy, w1_bf[:], w1_raw[:])
+
+        mx_tags = {t: f"y{own}" if t == LAST else f"mx{t}" for t in gather_order}
+        mx = {t: keep.tile([P, V], F32, name=f"mx{t}", tag=mx_tags[t], align_bytes=64) for t in gather_order}
+        mn = {t: keep.tile([P, V], F32, name=f"mn{t}", align_bytes=64) for t in (*early, own)}
+        for t in (LAST, own):
+            nc.vector.tensor_tensor(mx[t][:], ab[t][:, 0, :], ab[t][:, 1, :], ALU.max)
+        nc.vector.tensor_tensor(mn[own][:], ab[own][:, 0, :], ab[own][:, 1, :], ALU.min)
+        chosen = keep.tile([P, len(helped), 2, V], F32, name="chosen", tag=f"ab{own}", align_bytes=64)
+        rest = keep.tile([P, len(early), 2, V], F32, name="rest", align_bytes=64)
+        for n, t in enumerate(early):
+            nc.gpsimd.tensor_tensor(chosen[:, n], ab[t][:], weights[:, n], ALU.mult)
+            nc.gpsimd.tensor_tensor(mn[t][:], chosen[:, n, 0, :], chosen[:, n, 1, :], ALU.add)
+        for n, t in enumerate(early):
+            nc.gpsimd.tensor_tensor(rest[:, n], ab[t][:], chosen[:, n], ALU.subtract)
+            nc.gpsimd.tensor_tensor(mx[t][:], rest[:, n, 0, :], rest[:, n, 1, :], ALU.add)
+        last_slot = helped.index(LAST)
+        nc.gpsimd.tensor_tensor(chosen[:, last_slot], ab[LAST][:], weights[:, last_slot], ALU.mult)
+
+        z_both = keep.tile([P, H, PACK], BF16, name="z_both", tag="diff", align_bytes=64)
         z_bf = [z_both[:, h * HALF : (h + 1) * HALF, :] for h in range(2)]
         zs = [keep.tile([P, H], F32, name=f"zs{t}", tag=f"zs{t}", align_bytes=64) for t in range(PACK)]
-        w1_tags = ("mn0", "zs1")
+        w1_tags = (f"mx{early[0]}", f"zs{early[1]}")
         w1_codes = [keep.tile([P, HALF], U32, name=f"w1_codes{h}", tag=w1_tags[h], align_bytes=64) for h in range(2)]
         w1_plane = [keep.tile([P, HALF], U8, name=f"w1_plane{h}", align_bytes=64) for h in range(2)]
 
         def quantize_w1(h):
             quantize(nc, w1_codes[h][:], w1_plane[h][:], w1_bf[:, h * HALF : (h + 1) * HALF, :])
 
-        def scatter_mx(i):
-            nc.vector.tensor_copy(zs[order[i]][:].indirect(lb_sb[:]), mx[:, i, :])
+        def scatter(t, offsets, values):
+            nc.vector.tensor_copy(zs[t][:].indirect(offsets[:]), values[t][:])
 
-        def scatter_mn(i):
-            t = order[i]
-            nc.vector.tensor_copy(zs[t][:].indirect(la_sb[:]), mn[i][:])
-            for h in range(2) if t < LAST else [1]:
+        def round_z(t, halves):
+            for h in halves:
                 nc.scalar.activation(z_bf[h][:, :, t], zs[t][:, h * HALF : (h + 1) * HALF], COPY, scale=gate[:, t : t + 1])
 
-        scatter_mx(LAST)
-        scatter_mx(0)
-        scatter_mn(LAST)
-        last_gate = keep.tile([P, 1], F32, name="last_gate", tag=f"zs{LAST - 1}", align_bytes=64)
+        scatter(own, lb_sb, mx)
+        scatter(LAST, lb_sb, mx)
+        scatter(own, la_sb, mn)
+        round_z(own, range(2))
+        last_gate = keep.tile([P, 1], F32, name="last_gate", tag=f"zs{own}", align_bytes=64)
         nc.scalar.copy(last_gate[:], gate[:, LAST:])
-        for i in range(1, LAST):
-            scatter_mx(i)
-        for i in range(LAST):
-            scatter_mn(i)
+        for t in early:
+            scatter(t, la_sb, mn)
+        for t in early:
+            scatter(t, lb_sb, mx)
+            round_z(t, range(2))
+        nc.vector.tensor_tensor(zs[LAST][:].indirect(la_sb[:]), chosen[:, last_slot, 0, :], chosen[:, last_slot, 1, :], ALU.add)
+        round_z(LAST, [1])
 
         quarters = (slice(0, P), slice(P, HALF))
         whole_half = slice(0, HALF)

@@ -105,7 +105,7 @@ def tile_picked_mixscat_none_p_kernel(tc, x_words, x_scales, wa, gt, w1, offs, l
 
         early = (0, 1)
         own = LAST - 1
-        gather_order = (*early, LAST, own)
+        gather_order = tuple(range(PACK))
         helped = (*early, LAST)
 
         y = [keep.tile([P, H], F32, name=f"y{t}", tag=f"y{t}", align_bytes=64) for t in range(PACK)]
@@ -125,65 +125,91 @@ def tile_picked_mixscat_none_p_kernel(tc, x_words, x_scales, wa, gt, w1, offs, l
             nc.vector.tensor_copy(ab[t][:, 0, :], y[t][:].indirect(la_sb[:]))
             nc.vector.tensor_copy(ab[t][:, 1, :], y[t][:].indirect(lb_sb[:]))
 
-        diff = keep.tile([P, len(helped), V], F32, name="diff", tag="diff", align_bytes=64)
-        signs = keep.tile([P, len(helped), V], F32, name="signs", tag="signs", align_bytes=64)
-        weights = keep.tile([P, len(helped), 2, V], F32, name="weights", align_bytes=64)
-        for n, t in enumerate(helped):
-            nc.gpsimd.tensor_tensor(diff[:, n, :], ab[t][:, 0, :], ab[t][:, 1, :], ALU.subtract)
-            nc.scalar.activation(signs[:, n, :], diff[:, n, :], SIGN)
-            nc.scalar.activation(weights[:, n, 0, :], signs[:, n, :], COPY, scale=-0.5, bias=0.5)
-            nc.scalar.activation(weights[:, n, 1, :], signs[:, n, :], COPY, scale=0.5, bias=0.5)
-        w1_bf = keep.tile([P, N, PACK], BF16, name="w1_bf", tag="signs", align_bytes=64)
+        weights = {t: keep.tile([P, 2, V], F32, name=f"weights{t}", tag=f"weights{t}", align_bytes=64) for t in helped}
+
+        def weigh(t, diff):
+            signs = keep.tile([P, V], F32, name=f"signs{t}", tag="late_signs" if t == LAST else "early_signs", align_bytes=64)
+            nc.gpsimd.tensor_tensor(diff, ab[t][:, 0, :], ab[t][:, 1, :], ALU.subtract)
+            nc.scalar.activation(signs[:], diff, SIGN)
+            nc.scalar.activation(weights[t][:, 0, :], signs[:], COPY, scale=-0.5, bias=0.5)
+            nc.scalar.activation(weights[t][:, 1, :], signs[:], COPY, scale=0.5, bias=0.5)
+
+        for t in early:
+            diff = keep.tile([P, V], F32, name=f"diff{t}", tag=f"diff{t}", align_bytes=64)
+            weigh(t, diff[:])
+        first_chosen = keep.tile([P, 2, V], F32, name="first_chosen", align_bytes=64)
+        nc.gpsimd.tensor_tensor(first_chosen[:], ab[0][:], weights[0][:], ALU.mult)
+        w1_bf = keep.tile([P, N, PACK], BF16, name="w1_bf", tag="early_signs", align_bytes=64)
         interleave(nc.scalar.copy, w1_bf[:], w1_raw[:])
 
-        mx_tags = {t: f"y{own}" if t == LAST else f"mx{t}" for t in gather_order}
-        mx = {t: keep.tile([P, V], F32, name=f"mx{t}", tag=mx_tags[t], align_bytes=64) for t in gather_order}
-        mn = {t: keep.tile([P, V], F32, name=f"mn{t}", align_bytes=64) for t in (*early, own)}
-        for t in (LAST, own):
-            nc.vector.tensor_tensor(mx[t][:], ab[t][:, 0, :], ab[t][:, 1, :], ALU.max)
-        nc.vector.tensor_tensor(mn[own][:], ab[own][:, 0, :], ab[own][:, 1, :], ALU.min)
-        chosen = keep.tile([P, len(helped), 2, V], F32, name="chosen", tag=f"ab{own}", align_bytes=64)
-        rest = keep.tile([P, len(early), 2, V], F32, name="rest", align_bytes=64)
-        for n, t in enumerate(early):
-            nc.gpsimd.tensor_tensor(chosen[:, n], ab[t][:], weights[:, n], ALU.mult)
-            nc.gpsimd.tensor_tensor(mn[t][:], chosen[:, n, 0, :], chosen[:, n, 1, :], ALU.add)
-        for n, t in enumerate(early):
-            nc.gpsimd.tensor_tensor(rest[:, n], ab[t][:], chosen[:, n], ALU.subtract)
-            nc.gpsimd.tensor_tensor(mx[t][:], rest[:, n, 0, :], rest[:, n, 1, :], ALU.add)
-        last_slot = helped.index(LAST)
-        nc.gpsimd.tensor_tensor(chosen[:, last_slot], ab[LAST][:], weights[:, last_slot], ALU.mult)
+        own_pair = keep.tile([P, 2, V], F32, name="own_pair", tag=f"diff{early[1]}", align_bytes=64)
+        nc.vector.tensor_tensor(own_pair[:, 1, :], ab[own][:, 0, :], ab[own][:, 1, :], ALU.max)
+        nc.vector.tensor_tensor(own_pair[:, 0, :], ab[own][:, 0, :], ab[own][:, 1, :], ALU.min)
+        late = keep.tile([P, 4, 2, V], F32, name="late", tag=f"ab{own}", align_bytes=64)
+        chosen = {0: first_chosen[:], 1: late[:, 1], LAST: late[:, 2]}
+        rest = {0: late[:, 3]}
+        mn = {own: own_pair[:, 0, :], 0: late[:, 0, 0, :]}
+        mx = {own: own_pair[:, 1, :]}
+        for t in (1, LAST):
+            mn[t] = keep.tile([P, V], F32, name=f"mn{t}", align_bytes=64)[:]
+        for t in early:
+            mx[t] = keep.tile([P, V], F32, name=f"mx{t}", align_bytes=64)[:]
 
-        z_both = keep.tile([P, H, PACK], BF16, name="z_both", tag="diff", align_bytes=64)
+        def choose(t):
+            nc.gpsimd.tensor_tensor(chosen[t], ab[t][:], weights[t][:], ALU.mult)
+
+        def leave(t):
+            nc.gpsimd.tensor_tensor(rest[t], ab[t][:], chosen[t], ALU.subtract)
+
+        def join(result, pair):
+            nc.gpsimd.tensor_tensor(result, pair[:, 0, :], pair[:, 1, :], ALU.add)
+
+        join(mn[0], chosen[0])
+        weigh(LAST, late[:, 0, 1, :])
+        choose(1)
+        leave(0)
+        join(mn[1], chosen[1])
+        choose(LAST)
+        join(mx[0], rest[0])
+        join(mn[LAST], chosen[LAST])
+        rest[1] = keep.tile([P, 2, V], F32, name="second_rest", tag=f"weights{LAST}", align_bytes=64)[:]
+        leave(1)
+        join(mx[1], rest[1])
+        rest[LAST] = keep.tile([P, 2, V], F32, name="last_rest", tag="ab1", align_bytes=64)[:]
+        leave(LAST)
+
+        z_both = keep.tile([P, H, PACK], BF16, name="z_both", tag="late_signs", align_bytes=64)
         z_bf = [z_both[:, h * HALF : (h + 1) * HALF, :] for h in range(2)]
         zs = [keep.tile([P, H], F32, name=f"zs{t}", tag=f"zs{t}", align_bytes=64) for t in range(PACK)]
-        w1_tags = (f"mx{early[0]}", f"zs{early[1]}")
-        w1_codes = [keep.tile([P, HALF], U32, name=f"w1_codes{h}", tag=w1_tags[h], align_bytes=64) for h in range(2)]
+        w1_tags = (f"ab{LAST}", f"zs{own}")
         w1_plane = [keep.tile([P, HALF], U8, name=f"w1_plane{h}", align_bytes=64) for h in range(2)]
 
         def quantize_w1(h):
             quantize(nc, w1_codes[h][:], w1_plane[h][:], w1_bf[:, h * HALF : (h + 1) * HALF, :])
 
         def scatter(t, offsets, values):
-            nc.vector.tensor_copy(zs[t][:].indirect(offsets[:]), values[t][:])
+            nc.vector.tensor_copy(zs[t][:].indirect(offsets[:]), values[t])
 
         def round_z(t, halves):
             for h in halves:
                 nc.scalar.activation(z_bf[h][:, :, t], zs[t][:, h * HALF : (h + 1) * HALF], COPY, scale=gate[:, t : t + 1])
 
         scatter(own, lb_sb, mx)
-        scatter(LAST, lb_sb, mx)
         scatter(own, la_sb, mn)
         round_z(own, range(2))
         last_gate = keep.tile([P, 1], F32, name="last_gate", tag=f"zs{own}", align_bytes=64)
         nc.scalar.copy(last_gate[:], gate[:, LAST:])
-        for t in early:
-            scatter(t, la_sb, mn)
-        for t in early:
-            scatter(t, lb_sb, mx)
-            round_z(t, range(2))
-        nc.vector.tensor_tensor(zs[LAST][:].indirect(la_sb[:]), chosen[:, last_slot, 0, :], chosen[:, last_slot, 1, :], ALU.add)
+        scatter(0, la_sb, mn)
+        scatter(1, la_sb, mn)
+        scatter(0, lb_sb, mx)
+        round_z(0, range(2))
+        scatter(LAST, la_sb, mn)
+        scatter(1, lb_sb, mx)
+        round_z(1, range(2))
+        nc.vector.tensor_tensor(zs[LAST][:].indirect(lb_sb[:]), rest[LAST][:, 0, :], rest[LAST][:, 1, :], ALU.add)
         round_z(LAST, [1])
 
+        w1_codes = [keep.tile([P, HALF], U32, name=f"w1_codes{h}", tag=w1_tags[h], align_bytes=64) for h in range(2)]
         quarters = (slice(0, P), slice(P, HALF))
         whole_half = slice(0, HALF)
         quantize_w1(0)

@@ -1,6 +1,7 @@
 from contextlib import ExitStack
 
 import concourse.mybir as mybir
+from concourse.masks import make_identity
 
 K, T, S, V, N, H = 512, 2048, 512, 256, 512, 512
 FLOPS = 2 * K * S * H + 2 * S * N * H
@@ -103,10 +104,11 @@ def tile_picked_mixscat_none_p_kernel(tc, x_words, x_scales, wa, gt, w1, offs, l
         gate = keep.tile([P, PACK], F32, name="gate", tag="x_table", align_bytes=64)
         nc.sync.dma_start(gate[:], gt.rearrange("(p t) o -> p (t o)", t=PACK))
 
-        early = (0, 1)
         own = LAST - 1
-        gather_order = tuple(range(PACK))
-        helped = (*early, LAST)
+        gather_order = (0, own, 1, LAST)
+        helped = (0, 1, LAST)
+        identity = keep.tile([P, P], F32, name="identity", align_bytes=64)
+        make_identity(nc, identity[:])
 
         y = [keep.tile([P, H], F32, name=f"y{t}", tag=f"y{t}", align_bytes=64) for t in range(PACK)]
         first_tile_pieces = (
@@ -121,81 +123,102 @@ def tile_picked_mixscat_none_p_kernel(tc, x_words, x_scales, wa, gt, w1, offs, l
                 copy(y[t][:, cols], acc[:])
 
         ab = {t: keep.tile([P, 2, V], F32, name=f"ab{t}", tag=f"ab{t}", align_bytes=64) for t in gather_order}
-        for t in gather_order:
+
+        def fetch_a(t):
             nc.vector.tensor_copy(ab[t][:, 0, :], y[t][:].indirect(la_sb[:]))
-            nc.vector.tensor_copy(ab[t][:, 1, :], y[t][:].indirect(lb_sb[:]))
 
-        weights = {t: keep.tile([P, 2, V], F32, name=f"weights{t}", tag=f"weights{t}", align_bytes=64) for t in helped}
+        def fetch_minus_b(t):
+            nc.vector.tensor_scalar(ab[t][:, 1, :], y[t][:].indirect(lb_sb[:]), -1.0, 0.0, ALU.mult, ALU.add)
 
-        def weigh(t, diff):
-            signs = keep.tile([P, V], F32, name=f"signs{t}", tag="late_signs" if t == LAST else "early_signs", align_bytes=64)
-            nc.gpsimd.tensor_tensor(diff, ab[t][:, 0, :], ab[t][:, 1, :], ALU.subtract)
-            nc.scalar.activation(signs[:], diff, SIGN)
-            nc.scalar.activation(weights[t][:, 0, :], signs[:], COPY, scale=-0.5, bias=0.5)
-            nc.scalar.activation(weights[t][:, 1, :], signs[:], COPY, scale=0.5, bias=0.5)
+        weights = {t: keep.tile([P, 4, V], F32, name=f"weights{t}", align_bytes=64) for t in helped}
 
-        for t in early:
-            diff = keep.tile([P, V], F32, name=f"diff{t}", tag=f"diff{t}", align_bytes=64)
-            weigh(t, diff[:])
-        first_chosen = keep.tile([P, 2, V], F32, name="first_chosen", align_bytes=64)
-        nc.gpsimd.tensor_tensor(first_chosen[:], ab[0][:], weights[0][:], ALU.mult)
-        w1_bf = keep.tile([P, N, PACK], BF16, name="w1_bf", tag="early_signs", align_bytes=64)
-        interleave(nc.scalar.copy, w1_bf[:], w1_raw[:])
+        def weigh(t, signs):
+            for slot, half_sign, half in ((2, -0.5, 0.5), (3, -0.5, -0.5), (1, 0.5, 0.5)):
+                nc.scalar.activation(weights[t][:, slot, :], signs, COPY, scale=half_sign, bias=half)
 
-        own_pair = keep.tile([P, 2, V], F32, name="own_pair", tag=f"diff{early[1]}", align_bytes=64)
+        def signs_by_transposes(t):
+            turned = psum.tile([P, 2, P], F32, name="acc")
+            for c in range(2):
+                for i in range(2):
+                    nc.tensor.matmul(turned[:, c, :], ab[t][:, i, c * P : (c + 1) * P], identity[:], start=i == 0, stop=i == 1, is_transpose=True)
+            turned_signs = keep.tile([P, 2, P], F32, name=f"turned_signs{t}", tag=f"turned_signs{t}", align_bytes=64)
+            nc.scalar.activation(turned_signs[:], turned[:], SIGN)
+            signs = psum.tile([P, 2, P], F32, name="acc")
+            for c in range(2):
+                nc.tensor.transpose(signs[:, c, :], turned_signs[:, c, :], identity[:])
+            return signs[:].rearrange("p c m -> p (c m)")
+
+        fetch_a(0)
+        fetch_minus_b(0)
+        first_diff = keep.tile([P, V], F32, name="first_diff", align_bytes=64)
+        first_signs = keep.tile([P, V], F32, name="first_signs", align_bytes=64)
+        nc.gpsimd.tensor_tensor(first_diff[:], ab[0][:, 0, :], ab[0][:, 1, :], ALU.add)
+        nc.scalar.activation(first_signs[:], first_diff[:], SIGN)
+        weigh(0, first_signs[:])
+        fetch_a(own)
+        nc.vector.tensor_copy(ab[own][:, 1, :], y[own][:].indirect(lb_sb[:]))
+        fetch_a(1)
+        own_pair = keep.tile([P, 2, V], F32, name="own_pair", align_bytes=64)
         nc.vector.tensor_tensor(own_pair[:, 1, :], ab[own][:, 0, :], ab[own][:, 1, :], ALU.max)
         nc.vector.tensor_tensor(own_pair[:, 0, :], ab[own][:, 0, :], ab[own][:, 1, :], ALU.min)
-        late = keep.tile([P, 4, 2, V], F32, name="late", tag=f"ab{own}", align_bytes=64)
-        chosen = {0: first_chosen[:], 1: late[:, 1], LAST: late[:, 2]}
-        rest = {0: late[:, 3]}
-        mn = {own: own_pair[:, 0, :], 0: late[:, 0, 0, :]}
-        mx = {own: own_pair[:, 1, :]}
-        for t in (1, LAST):
-            mn[t] = keep.tile([P, V], F32, name=f"mn{t}", align_bytes=64)[:]
-        for t in early:
-            mx[t] = keep.tile([P, V], F32, name=f"mx{t}", align_bytes=64)[:]
+        fetch_minus_b(1)
+        weigh(1, signs_by_transposes(1))
+        fetch_a(LAST)
 
-        def choose(t):
-            nc.gpsimd.tensor_tensor(chosen[t], ab[t][:], weights[t][:], ALU.mult)
-
-        def leave(t):
-            nc.gpsimd.tensor_tensor(rest[t], ab[t][:], chosen[t], ALU.subtract)
-
-        def join(result, pair):
-            nc.gpsimd.tensor_tensor(result, pair[:, 0, :], pair[:, 1, :], ALU.add)
-
-        join(mn[0], chosen[0])
-        weigh(LAST, late[:, 0, 1, :])
-        choose(1)
-        leave(0)
-        join(mn[1], chosen[1])
-        choose(LAST)
-        join(mx[0], rest[0])
-        join(mn[LAST], chosen[LAST])
-        rest[1] = keep.tile([P, 2, V], F32, name="second_rest", tag=f"weights{LAST}", align_bytes=64)[:]
-        leave(1)
-        join(mx[1], rest[1])
-        rest[LAST] = keep.tile([P, 2, V], F32, name="last_rest", tag="ab1", align_bytes=64)[:]
-        leave(LAST)
-
-        z_both = keep.tile([P, H, PACK], BF16, name="z_both", tag="late_signs", align_bytes=64)
-        z_bf = [z_both[:, h * HALF : (h + 1) * HALF, :] for h in range(2)]
         zs = [keep.tile([P, H], F32, name=f"zs{t}", tag=f"zs{t}", align_bytes=64) for t in range(PACK)]
+        mn = {own: own_pair[:, 0, :]}
+        mx = {own: own_pair[:, 1, :]}
+
+        def scatter(t, offsets, values):
+            nc.vector.tensor_copy(zs[t][:].indirect(offsets[:]), values[t])
+
+        scatter(own, lb_sb, mx)
+        fetch_minus_b(LAST)
+        weigh(LAST, signs_by_transposes(LAST))
+        scatter(own, la_sb, mn)
+        w1_bf = keep.tile([P, N, PACK], BF16, name="w1_bf", tag=f"turned_signs{LAST}", align_bytes=64)
+        interleave(nc.scalar.copy, w1_bf[:], w1_raw[:])
+
+        first_terms = keep.tile([P, 2, 2, V], F32, name="first_terms", tag=f"ab{own}", align_bytes=64)
+        low = {0: first_terms[:, 0], 1: keep.tile([P, 2, V], F32, name="low1", align_bytes=64)[:]}
+        high = {0: first_terms[:, 1], 1: weights[LAST][:, :2, :], LAST: keep.tile([P, 2, V], F32, name="high_last", align_bytes=64)[:]}
+        mx[0] = weights[1][:, 3, :]
+        for t in helped[1:]:
+            mx[t] = keep.tile([P, V], F32, name=f"mx{t}", align_bytes=64)[:]
+        for t in helped[:2]:
+            mn[t] = keep.tile([P, V], F32, name=f"mn{t}", align_bytes=64)[:]
+
+        def low_terms(t):
+            nc.gpsimd.tensor_tensor(low[t], ab[t][:], weights[t][:, 2:, :], ALU.mult)
+
+        def make_min(t):
+            low_terms(t)
+            nc.gpsimd.tensor_tensor(mn[t], low[t][:, 0, :], low[t][:, 1, :], ALU.add)
+
+        def make_max(t):
+            nc.gpsimd.tensor_tensor(high[t], ab[t][:], weights[t][:, 1:3, :], ALU.mult)
+            nc.gpsimd.tensor_tensor(mx[t], high[t][:, 0, :], high[t][:, 1, :], ALU.subtract)
+
+        make_min(0)
+        make_min(1)
+        make_max(0)
+        make_max(LAST)
+        make_max(1)
+        low[LAST] = keep.tile([P, 2, V], F32, name="low_last", tag="ab1", align_bytes=64)[:]
+        low_terms(LAST)
+
+        z_both = keep.tile([P, H, PACK], BF16, name="z_both", tag="wa_raw1", align_bytes=64)
+        z_bf = [z_both[:, h * HALF : (h + 1) * HALF, :] for h in range(2)]
         w1_tags = (f"ab{LAST}", f"zs{own}")
         w1_plane = [keep.tile([P, HALF], U8, name=f"w1_plane{h}", align_bytes=64) for h in range(2)]
 
         def quantize_w1(h):
             quantize(nc, w1_codes[h][:], w1_plane[h][:], w1_bf[:, h * HALF : (h + 1) * HALF, :])
 
-        def scatter(t, offsets, values):
-            nc.vector.tensor_copy(zs[t][:].indirect(offsets[:]), values[t])
-
         def round_z(t, halves):
             for h in halves:
                 nc.scalar.activation(z_bf[h][:, :, t], zs[t][:, h * HALF : (h + 1) * HALF], COPY, scale=gate[:, t : t + 1])
 
-        scatter(own, lb_sb, mx)
-        scatter(own, la_sb, mn)
         round_z(own, range(2))
         last_gate = keep.tile([P, 1], F32, name="last_gate", tag=f"zs{own}", align_bytes=64)
         nc.scalar.copy(last_gate[:], gate[:, LAST:])
@@ -203,10 +226,10 @@ def tile_picked_mixscat_none_p_kernel(tc, x_words, x_scales, wa, gt, w1, offs, l
         scatter(1, la_sb, mn)
         scatter(0, lb_sb, mx)
         round_z(0, range(2))
-        scatter(LAST, la_sb, mn)
+        scatter(LAST, lb_sb, mx)
         scatter(1, lb_sb, mx)
         round_z(1, range(2))
-        nc.vector.tensor_tensor(zs[LAST][:].indirect(lb_sb[:]), rest[LAST][:, 0, :], rest[LAST][:, 1, :], ALU.add)
+        nc.vector.tensor_tensor(zs[LAST][:].indirect(la_sb[:]), low[LAST][:, 0, :], low[LAST][:, 1, :], ALU.add)
         round_z(LAST, [1])
 
         w1_codes = [keep.tile([P, HALF], U32, name=f"w1_codes{h}", tag=w1_tags[h], align_bytes=64) for h in range(2)]

@@ -23,7 +23,6 @@ HALF = 256
 LAST = PACK - 1
 BANKS = 8
 SCALE_ROWS = K // 32
-SCALAR_COLUMNS = ((256, 64), (80, 80))
 
 
 def interleave(copy, grouped, raw):
@@ -60,15 +59,17 @@ def tile_picked_mixscat_none_p_kernel(tc, x_words, x_scales, wa, gt, w1, offs, l
         lb_sb = keep.tile([P, V // 16], U16, name="lb_sb")
         x_table = keep.tile([P, T], I32, name="x_table", tag="x_table", align_bytes=64)
         s_table = keep.tile([P, T], U8, name="s_table", align_bytes=64)
-        wa_raw = [keep.tile([P, 2, H], F32, name=f"wa_raw{i}", tag=f"wa_raw{i}", align_bytes=64) for i in range(2)]
+        wa_first = keep.tile([P, 2, H], F32, name="wa_first", align_bytes=64)
+        wa_second = [keep.tile([P, 2, HALF], F32, name=f"wa_second{h}", tag=f"wa_second{h}", align_bytes=64) for h in range(2)]
 
         s_rows = keep.tile([P, T // 4], I32, name="s_rows", align_bytes=64)
         nc.sync.dma_start(offs_sb[:], offs)
         nc.scalar.dma_start(s_rows[:SCALE_ROWS, :], x_scales[0].bitcast(I32))
         nc.sync.dma_start(x_table[:], x_words[0].rearrange("p n r -> p (n r)").bitcast(I32))
         wa_rows = wa.rearrange("(p j) n -> p j n", j=PACK)
-        for i in range(2):
-            nc.sync.dma_start(wa_raw[i][:], wa_rows[:, 2 * i : 2 * i + 2, :])
+        nc.sync.dma_start(wa_first[:], wa_rows[:, :2, :])
+        for h in range(2):
+            nc.sync.dma_start(wa_second[h][:], wa_rows[:, 2:, h * HALF : (h + 1) * HALF])
         nc.sync.dma_start(la_sb[:], la)
         nc.sync.dma_start(lb_sb[:], lb)
 
@@ -86,20 +87,30 @@ def tile_picked_mixscat_none_p_kernel(tc, x_words, x_scales, wa, gt, w1, offs, l
 
         wa_codes = keep.tile([P, H], U32, name="wa_codes", align_bytes=64)
         wa_plane = keep.tile([P, H], U8, name="wa_plane", align_bytes=64)
-        wa_bf = [keep.tile([P, HALF, PACK], BF16, name=f"wa_bf{h}", align_bytes=64) for h in range(2)]
-        for i in range(2):
-            places = slice(2 * i, 2 * i + 2)
-            for h in range(2):
-                cut = SCALAR_COLUMNS[i][h]
-                raw = wa_raw[i][:, :, h * HALF : (h + 1) * HALF]
-                interleave(nc.scalar.copy, wa_bf[h][:, :cut, places], raw[:, :, :cut])
-                if cut < HALF:
-                    interleave(nc.vector.tensor_copy, wa_bf[h][:, cut:, places], raw[:, :, cut:])
-        for h in range(2):
-            cols = slice(h * HALF, (h + 1) * HALF)
-            quantize(nc, wa_codes[:, cols], wa_plane[:, cols], wa_bf[h][:])
+        wa_bf = [keep.tile([P, P, PACK], BF16, name=f"wa_bf{q}", align_bytes=64) for q in range(4)]
 
-        w1_raw = keep.tile([P, PACK, N], F32, name="w1_raw", tag="wa_raw1", align_bytes=64)
+        def round_first(copy, q):
+            interleave(copy, wa_bf[q][:, :, :2], wa_first[:, :, q * P : (q + 1) * P])
+
+        def round_second(copy, q):
+            interleave(copy, wa_bf[q][:, :, 2:], wa_second[q // 2][:, :, q % 2 * P : (q % 2 + 1) * P])
+
+        def quantize_wa(q):
+            quantize(nc, wa_codes[:, q * P : (q + 1) * P], wa_plane[:, q * P : (q + 1) * P], wa_bf[q][:])
+
+        for q in range(3):
+            round_first(nc.scalar.copy, q)
+        round_first(nc.vector.tensor_copy, 3)
+        for q in range(2):
+            round_second(nc.vector.tensor_copy, q)
+        for q in range(2):
+            quantize_wa(q)
+        round_second(nc.scalar.copy, 2)
+        round_second(nc.vector.tensor_copy, 3)
+        for q in range(2, 4):
+            quantize_wa(q)
+
+        w1_raw = keep.tile([P, PACK, N], F32, name="w1_raw", tag="wa_second1", align_bytes=64)
         nc.sync.dma_start(w1_raw[:], w1.rearrange("(p j) n -> p j n", j=PACK))
         gate = keep.tile([P, PACK], F32, name="gate", tag="x_table", align_bytes=64)
         nc.sync.dma_start(gate[:], gt.rearrange("(p t) o -> p (t o)", t=PACK))
@@ -207,7 +218,7 @@ def tile_picked_mixscat_none_p_kernel(tc, x_words, x_scales, wa, gt, w1, offs, l
         low[LAST] = keep.tile([P, 2, V], F32, name="low_last", tag="ab1", align_bytes=64)[:]
         low_terms(LAST)
 
-        z_both = keep.tile([P, H, PACK], BF16, name="z_both", tag="wa_raw1", align_bytes=64)
+        z_both = keep.tile([P, H, PACK], BF16, name="z_both", tag="wa_second1", align_bytes=64)
         z_bf = [z_both[:, h * HALF : (h + 1) * HALF, :] for h in range(2)]
         w1_tags = (f"ab{LAST}", f"zs{own}")
         w1_plane = [keep.tile([P, HALF], U8, name=f"w1_plane{h}", align_bytes=64) for h in range(2)]

@@ -73,6 +73,10 @@ def tile_picked_mixscat_none_p_kernel(tc, x_words, x_scales, wa, gt, w1, offs, l
         nc.sync.dma_start(la_sb[:], la)
         nc.sync.dma_start(lb_sb[:], lb)
 
+        warm = keep.tile([P, 2], F32, name="warm", align_bytes=64)
+        nc.vector.memset(warm[:, :1], 0.0)
+        nc.scalar.copy(warm[:, 1:], warm[:, :1])
+
         nc.vector.memset(s_table[:].bitcast(I32), 0)
         nc.vector.tensor_copy(s_table[:SCALE_ROWS, :].bitcast(I32), s_rows[:SCALE_ROWS, :])
         s_picked = keep.tile([P, S], U8, name="s_picked", align_bytes=64)
@@ -81,7 +85,7 @@ def tile_picked_mixscat_none_p_kernel(tc, x_words, x_scales, wa, gt, w1, offs, l
         nc.vector.tensor_copy(x_planes[:], s_picked[:].rearrange("p (m t) -> p t m", t=PACK))
         plane_words = x_planes[:].rearrange("p t m -> p (t m)").bitcast(I32)
         for q in range(1, 4):
-            nc.sync.dma_start(plane_words[32 * q : 32 * q + 4, :], plane_words[4 * q : 4 * q + 4, :])
+            nc.scalar.dma_start(plane_words[32 * q : 32 * q + 4, :], plane_words[4 * q : 4 * q + 4, :])
         x_codes = keep.tile([P, PACK, P], U32, name="x_codes", align_bytes=64)
         nc.vector.tensor_copy(x_codes[:].rearrange("p t m -> p m t"), x_table[:].bitcast(U32).indirect(offs_sb[:]))
 

@@ -62,9 +62,8 @@ def tile_picked_mixscat_none_p_kernel(tc, x_words, x_scales, wa, gt, w1, offs, l
         wa_first = keep.tile([P, 2, H], F32, name="wa_first", align_bytes=64)
         wa_second = [keep.tile([P, 2, HALF], F32, name=f"wa_second{h}", tag=f"wa_second{h}", align_bytes=64) for h in range(2)]
 
-        s_rows = keep.tile([P, T // 4], I32, name="s_rows", align_bytes=64)
         nc.sync.dma_start(offs_sb[:], offs)
-        nc.scalar.dma_start(s_rows[:SCALE_ROWS, :], x_scales[0].bitcast(I32))
+        nc.scalar.dma_start(s_table[P - SCALE_ROWS :, :].bitcast(I32), x_scales[0].bitcast(I32))
         nc.sync.dma_start(x_table[:], x_words[0].rearrange("p n r -> p (n r)").bitcast(I32))
         wa_rows = wa.rearrange("(p j) n -> p j n", j=PACK)
         nc.sync.dma_start(wa_first[:], wa_rows[:, :2, :])
@@ -77,15 +76,15 @@ def tile_picked_mixscat_none_p_kernel(tc, x_words, x_scales, wa, gt, w1, offs, l
         nc.vector.memset(warm[:, :1], 0.0)
         nc.scalar.copy(warm[:, 1:], warm[:, :1])
 
-        nc.vector.memset(s_table[:].bitcast(I32), 0)
-        nc.vector.tensor_copy(s_table[:SCALE_ROWS, :].bitcast(I32), s_rows[:SCALE_ROWS, :])
+        nc.vector.memset(s_table[: P - SCALE_ROWS, :].bitcast(I32), 0)
         s_picked = keep.tile([P, S], U8, name="s_picked", align_bytes=64)
         nc.vector.tensor_copy(s_picked[:], s_table[:].indirect(offs_sb[:]))
         x_planes = keep.tile([P, PACK, P], U8, name="x_planes", align_bytes=64)
         nc.vector.tensor_copy(x_planes[:], s_picked[:].rearrange("p (m t) -> p t m", t=PACK))
         plane_words = x_planes[:].rearrange("p t m -> p (t m)").bitcast(I32)
-        for q in range(1, 4):
-            nc.scalar.dma_start(plane_words[32 * q : 32 * q + 4, :], plane_words[4 * q : 4 * q + 4, :])
+        for q in range(4):
+            first = P - SCALE_ROWS + 4 * q
+            nc.scalar.dma_start(plane_words[32 * q : 32 * q + 4, :], plane_words[first : first + 4, :])
         x_codes = keep.tile([P, PACK, P], U32, name="x_codes", align_bytes=64)
         nc.vector.tensor_copy(x_codes[:].rearrange("p t m -> p m t"), x_table[:].bitcast(U32).indirect(offs_sb[:]))
 

@@ -1,7 +1,6 @@
 from contextlib import ExitStack
 
 import concourse.mybir as mybir
-from concourse.masks import make_identity
 
 K, T, S, V, N, H = 512, 2048, 512, 256, 512, 512
 FLOPS = 2 * K * S * H + 2 * S * N * H
@@ -15,13 +14,15 @@ U8 = mybir.dt.uint8
 FP8X4 = mybir.dt.float8_e4m3fn_x4
 ALU = mybir.AluOpType
 COPY = mybir.ActivationFunctionType.Copy
-SIGN = mybir.ActivationFunctionType.Sign
 
 P = 128
 PACK = 4
 HALF = 256
 LAST = PACK - 1
 BANKS = 8
+KIB = 1024
+W1_RAW_AT = 0
+LAST_Y_AT = 8 * KIB
 SCALE_ROWS = K // 32
 
 
@@ -52,7 +53,8 @@ def tile_picked_mixscat_none_p_kernel(tc, x_words, x_scales, wa, gt, w1, offs, l
     nc = tc.nc
     with ExitStack() as ctx:
         keep = ctx.enter_context(tc.tile_pool(name="keep", bufs=1))
-        psum = ctx.enter_context(tc.psum_pool(name="psum", bufs=BANKS))
+        shared = ctx.enter_context(tc.tile_pool(name="shared", bufs=1))
+        psum = ctx.enter_context(tc.psum_pool(name="psum", bufs=1))
 
         offs_sb = keep.tile([P, S // 16], U16, name="offs_sb")
         la_sb = keep.tile([P, V // 16], U16, name="la_sb")
@@ -60,7 +62,10 @@ def tile_picked_mixscat_none_p_kernel(tc, x_words, x_scales, wa, gt, w1, offs, l
         x_table = keep.tile([P, T], I32, name="x_table", tag="x_table", align_bytes=64)
         s_table = keep.tile([P, T], U8, name="s_table", align_bytes=64)
         wa_first = keep.tile([P, 2, H], F32, name="wa_first", align_bytes=64)
-        wa_second = [keep.tile([P, 2, HALF], F32, name=f"wa_second{h}", tag=f"wa_second{h}", align_bytes=64) for h in range(2)]
+        wa_second = [
+            keep.tile([P, 2, HALF], F32, name="wa_second0", align_bytes=64),
+            shared.tile([P, 2, HALF], F32, name="wa_second1", offset=W1_RAW_AT, align_bytes=64),
+        ]
 
         nc.sync.dma_start(offs_sb[:], offs)
         nc.scalar.dma_start(s_table[P - SCALE_ROWS :, :].bitcast(I32), x_scales[0].bitcast(I32))
@@ -113,150 +118,103 @@ def tile_picked_mixscat_none_p_kernel(tc, x_words, x_scales, wa, gt, w1, offs, l
         for q in range(2, 4):
             quantize_wa(q)
 
-        w1_raw = keep.tile([P, PACK, N], F32, name="w1_raw", tag="wa_second1", align_bytes=64)
+        w1_raw = shared.tile([P, PACK, N], F32, name="w1_raw", offset=W1_RAW_AT, align_bytes=64)
         nc.sync.dma_start(w1_raw[:], w1.rearrange("(p j) n -> p j n", j=PACK))
         gate = keep.tile([P, PACK], F32, name="gate", tag="x_table", align_bytes=64)
         nc.sync.dma_start(gate[:], gt.rearrange("(p t) o -> p (t o)", t=PACK))
 
-        own = LAST - 1
-        gather_order = (0, own, 1, LAST)
-        helped = (0, 1, LAST)
-        identity = keep.tile([P, P], F32, name="identity", align_bytes=64)
-        make_identity(nc, identity[:])
+        order = (LAST - 1, 0, 1, LAST)
+        first = order[0]
 
-        y = [keep.tile([P, H], F32, name=f"y{t}", tag=f"y{t}", align_bytes=64) for t in range(PACK)]
-        first_tile_pieces = (
-            (slice(0, HALF), nc.scalar.copy),
-            (slice(HALF, HALF + P), nc.vector.tensor_copy),
-            (slice(HALF + P, H), nc.scalar.copy),
-        )
-        for t in gather_order:
-            for cols, copy in first_tile_pieces if t == gather_order[0] else [(slice(0, H), nc.scalar.copy)]:
-                acc = psum.tile([P, cols.stop - cols.start], F32, name="acc")
-                multiply(nc, acc[:], x_codes[:, t, :], x_planes[:, t, :], wa_codes[:, cols], wa_plane[:, cols])
-                copy(y[t][:, cols], acc[:])
+        y = {t: keep.tile([P, H], F32, name=f"y{t}", tag=f"y{t}", align_bytes=64) for t in order[:-1]}
+        y[LAST] = shared.tile([P, H], F32, name="y_last", offset=LAST_Y_AT, align_bytes=64)
+        a = {t: keep.tile([P, V], F32, name=f"a{t}", tag=f"a{t}", align_bytes=64) for t in order}
+        b = {t: keep.tile([P, V], F32, name=f"b{t}", tag=f"b{t}", align_bytes=64) for t in order}
 
-        ab = {t: keep.tile([P, 2, V], F32, name=f"ab{t}", tag=f"ab{t}", align_bytes=64) for t in gather_order}
+        def project(t, cols, bank, copy):
+            acc = psum.tile([P, cols.stop - cols.start], F32, name="acc", tag=f"bank{bank}")
+            multiply(nc, acc[:], x_codes[:, t, :], x_planes[:, t, :], wa_codes[:, cols], wa_plane[:, cols])
+            copy(y[t][:, cols], acc[:])
 
-        def fetch_a(t):
-            nc.vector.tensor_copy(ab[t][:, 0, :], y[t][:].indirect(la_sb[:]))
+        def fetch(values, t, offsets):
+            nc.scalar.activation(values[t][:], y[t][:].indirect(offsets[:]), COPY)
 
-        def fetch_minus_b(t):
-            nc.vector.tensor_scalar(ab[t][:, 1, :], y[t][:].indirect(lb_sb[:]), -1.0, 0.0, ALU.mult, ALU.add)
+        project(first, slice(0, HALF), 0, nc.scalar.copy)
+        project(first, slice(HALF, HALF + P), 1, nc.vector.tensor_copy)
+        project(first, slice(HALF + P, H), 2, nc.scalar.copy)
+        nc.vector.tensor_copy(a[first][:], y[first][:].indirect(la_sb[:]))
+        fetch(b, first, lb_sb)
+        for t in order[1:]:
+            project(t, slice(0, H), 2, nc.scalar.copy)
+            fetch(a, t, la_sb)
+            fetch(b, t, lb_sb)
 
-        weights = {t: keep.tile([P, 4, V], F32, name=f"weights{t}", align_bytes=64) for t in helped}
-
-        def weigh(t, signs):
-            for slot, half_sign, half in ((2, -0.5, 0.5), (3, -0.5, -0.5), (1, 0.5, 0.5)):
-                nc.scalar.activation(weights[t][:, slot, :], signs, COPY, scale=half_sign, bias=half)
-
-        def signs_by_transposes(t):
-            turned = psum.tile([P, 2, P], F32, name="acc")
-            for c in range(2):
-                for i in range(2):
-                    nc.tensor.matmul(turned[:, c, :], ab[t][:, i, c * P : (c + 1) * P], identity[:], start=i == 0, stop=i == 1, is_transpose=True)
-            turned_signs = keep.tile([P, 2, P], F32, name=f"turned_signs{t}", tag=f"turned_signs{t}", align_bytes=64)
-            nc.scalar.activation(turned_signs[:], turned[:], SIGN)
-            signs = psum.tile([P, 2, P], F32, name="acc")
-            for c in range(2):
-                nc.tensor.transpose(signs[:, c, :], turned_signs[:, c, :], identity[:])
-            return signs[:].rearrange("p c m -> p (c m)")
-
-        fetch_a(0)
-        fetch_minus_b(0)
-        first_diff = keep.tile([P, V], F32, name="first_diff", align_bytes=64)
-        first_signs = keep.tile([P, V], F32, name="first_signs", align_bytes=64)
-        nc.gpsimd.tensor_tensor(first_diff[:], ab[0][:, 0, :], ab[0][:, 1, :], ALU.add)
-        nc.scalar.activation(first_signs[:], first_diff[:], SIGN)
-        weigh(0, first_signs[:])
-        fetch_a(own)
-        nc.vector.tensor_copy(ab[own][:, 1, :], y[own][:].indirect(lb_sb[:]))
-        fetch_a(1)
-        own_pair = keep.tile([P, 2, V], F32, name="own_pair", align_bytes=64)
-        nc.vector.tensor_tensor(own_pair[:, 1, :], ab[own][:, 0, :], ab[own][:, 1, :], ALU.max)
-        nc.vector.tensor_tensor(own_pair[:, 0, :], ab[own][:, 0, :], ab[own][:, 1, :], ALU.min)
-        fetch_minus_b(1)
-        weigh(1, signs_by_transposes(1))
-        fetch_a(LAST)
-
-        zs = [keep.tile([P, H], F32, name=f"zs{t}", tag=f"zs{t}", align_bytes=64) for t in range(PACK)]
-        mn = {own: own_pair[:, 0, :]}
-        mx = {own: own_pair[:, 1, :]}
-
-        def scatter(t, offsets, values):
-            nc.vector.tensor_copy(zs[t][:].indirect(offsets[:]), values[t])
-
-        scatter(own, lb_sb, mx)
-        fetch_minus_b(LAST)
-        weigh(LAST, signs_by_transposes(LAST))
-        scatter(own, la_sb, mn)
-        w1_bf = keep.tile([P, N, PACK], BF16, name="w1_bf", tag=f"turned_signs{LAST}", align_bytes=64)
+        w1_bf = shared.tile([P, N, PACK], BF16, name="w1_bf", offset=LAST_Y_AT + KIB, align_bytes=64)
         interleave(nc.scalar.copy, w1_bf[:], w1_raw[:])
 
-        first_terms = keep.tile([P, 2, 2, V], F32, name="first_terms", tag=f"ab{own}", align_bytes=64)
-        low = {0: first_terms[:, 0], 1: keep.tile([P, 2, V], F32, name="low1", align_bytes=64)[:]}
-        high = {0: first_terms[:, 1], 1: weights[LAST][:, :2, :], LAST: keep.tile([P, 2, V], F32, name="high_last", align_bytes=64)[:]}
-        mx[0] = weights[1][:, 3, :]
-        for t in helped[1:]:
-            mx[t] = keep.tile([P, V], F32, name=f"mx{t}", align_bytes=64)[:]
-        for t in helped[:2]:
-            mn[t] = keep.tile([P, V], F32, name=f"mn{t}", align_bytes=64)[:]
-
-        def low_terms(t):
-            nc.gpsimd.tensor_tensor(low[t], ab[t][:], weights[t][:, 2:, :], ALU.mult)
-
-        def make_min(t):
-            low_terms(t)
-            nc.gpsimd.tensor_tensor(mn[t], low[t][:, 0, :], low[t][:, 1, :], ALU.add)
-
-        def make_max(t):
-            nc.gpsimd.tensor_tensor(high[t], ab[t][:], weights[t][:, 1:3, :], ALU.mult)
-            nc.gpsimd.tensor_tensor(mx[t], high[t][:, 0, :], high[t][:, 1, :], ALU.subtract)
-
-        make_min(0)
-        make_min(1)
-        make_max(0)
-        make_max(LAST)
-        make_max(1)
-        low[LAST] = keep.tile([P, 2, V], F32, name="low_last", tag="ab1", align_bytes=64)[:]
-        low_terms(LAST)
-
-        z_both = keep.tile([P, H, PACK], BF16, name="z_both", tag="wa_second1", align_bytes=64)
+        zs = {t: keep.tile([P, H], F32, name=f"zs{t}", tag=f"zs{t}", align_bytes=64) for t in order}
+        mn = {t: keep.tile([P, V], F32, name=f"mn{t}", align_bytes=64) for t in order}
+        mx = {t: keep.tile([P, V], F32, name=f"mx{t}", tag=f"y{later}", align_bytes=64) for t, later in zip(order[:2], order[1:])}
+        mx[order[2]] = shared.tile([P, V], F32, name="mx_third", offset=LAST_Y_AT, align_bytes=64)
+        mx[LAST] = shared.tile([P, V], F32, name="mx_last", offset=W1_RAW_AT + 4 * KIB, align_bytes=64)
+        z_both = shared.tile([P, H, PACK], BF16, name="z_both", offset=W1_RAW_AT, align_bytes=64)
         z_bf = [z_both[:, h * HALF : (h + 1) * HALF, :] for h in range(2)]
-        w1_tags = (f"ab{LAST}", f"zs{own}")
-        w1_plane = [keep.tile([P, HALF], U8, name=f"w1_plane{h}", align_bytes=64) for h in range(2)]
 
-        def quantize_w1(h):
-            quantize(nc, w1_codes[h][:], w1_plane[h][:], w1_bf[:, h * HALF : (h + 1) * HALF, :])
+        def take_min(t):
+            nc.vector.tensor_tensor(mn[t][:], a[t][:], b[t][:], ALU.min)
+
+        def take_max(t):
+            nc.vector.tensor_tensor(mx[t][:], a[t][:], b[t][:], ALU.max)
+
+        def put_min(t):
+            nc.vector.tensor_copy(zs[t][:].indirect(la_sb[:]), mn[t][:])
+
+        def put_max(t):
+            nc.vector.tensor_copy(zs[t][:].indirect(lb_sb[:]), mx[t][:])
 
         def round_z(t, halves):
             for h in halves:
                 nc.scalar.activation(z_bf[h][:, :, t], zs[t][:, h * HALF : (h + 1) * HALF], COPY, scale=gate[:, t : t + 1])
 
-        round_z(own, range(2))
-        last_gate = keep.tile([P, 1], F32, name="last_gate", tag=f"zs{own}", align_bytes=64)
-        nc.scalar.copy(last_gate[:], gate[:, LAST:])
-        scatter(0, la_sb, mn)
-        scatter(1, la_sb, mn)
-        scatter(0, lb_sb, mx)
-        round_z(0, range(2))
-        scatter(LAST, lb_sb, mx)
-        scatter(1, lb_sb, mx)
-        round_z(1, range(2))
-        nc.vector.tensor_tensor(zs[LAST][:].indirect(la_sb[:]), low[LAST][:, 0, :], low[LAST][:, 1, :], ALU.add)
+        w1_plane = [keep.tile([P, HALF], U8, name=f"w1_plane{h}", align_bytes=64) for h in range(2)]
+        w1_codes = [
+            keep.tile([P, HALF], U32, name="w1_codes0", align_bytes=64),
+            keep.tile([P, HALF], U32, name="w1_codes1", tag=f"a{LAST}", align_bytes=64),
+        ]
+
+        def quantize_w1(h):
+            quantize(nc, w1_codes[h][:], w1_plane[h][:], w1_bf[:, h * HALF : (h + 1) * HALF, :])
+
+        take_min(first)
+        put_min(first)
+        for earlier, t in zip(order[:2], order[1:3]):
+            take_min(t)
+            take_max(earlier)
+            put_min(t)
+            put_max(earlier)
+            round_z(earlier, range(2))
+            if earlier == first:
+                last_gate = keep.tile([P, 1], F32, name="last_gate", tag=f"zs{first}", align_bytes=64)
+                nc.scalar.copy(last_gate[:], gate[:, LAST:])
+        take_max(order[2])
+        take_min(LAST)
+        put_max(order[2])
+        put_min(LAST)
+        round_z(order[2], range(2))
+        take_max(LAST)
+        quantize_w1(0)
+        put_max(LAST)
+        quantize_w1(1)
         round_z(LAST, [1])
 
-        w1_codes = [keep.tile([P, HALF], U32, name=f"w1_codes{h}", tag=w1_tags[h], align_bytes=64) for h in range(2)]
         quarters = (slice(0, P), slice(P, HALF))
         whole_half = slice(0, HALF)
-        quantize_w1(0)
         for cols in quarters:
             nc.vector.tensor_scalar(z_bf[0][:, cols, LAST], zs[LAST][:, cols], last_gate[:], None, ALU.mult)
         z_codes = [keep.tile([P, HALF], U32, name=f"z_codes{h}", align_bytes=64) for h in range(2)]
         z_plane = [keep.tile([P, HALF], U8, name=f"z_plane{h}", align_bytes=64) for h in range(2)]
         for cols in quarters:
             quantize(nc, z_codes[0][:, cols], z_plane[0][:, cols], z_bf[0][:, cols, :])
-        quantize_w1(1)
         quantize(nc, z_codes[1][:], z_plane[1][:], z_bf[1])
 
         def mix(acc, h, m, cols):
@@ -264,11 +222,12 @@ def tile_picked_mixscat_none_p_kernel(tc, x_words, x_scales, wa, gt, w1, offs, l
             multiply(nc, acc, w1_codes[m // 2][:, places], w1_plane[m // 2][:, places], z_codes[h][:, cols], z_plane[h][:, cols])
 
         copies = (nc.scalar.copy, nc.vector.tensor_copy)
+        banks = list(range(BANKS)) + [0]
         for h in range(2):
             for m in range(N // P):
                 result = keep.tile([P, HALF], F32, name=f"result{h}{m}", align_bytes=64)
                 for cols in quarters if h == m == 0 else [whole_half]:
-                    acc = psum.tile([P, cols.stop - cols.start], F32, name="acc")
+                    acc = psum.tile([P, cols.stop - cols.start], F32, name="acc", tag=f"bank{banks.pop(0)}")
                     mix(acc[:], h, m, cols)
                     copies[m % 2](result[:, cols], acc[:])
                 nc.sync.dma_start(out[m * P : (m + 1) * P, h * HALF : (h + 1) * HALF], result[:])

@@ -14,6 +14,7 @@ U8 = mybir.dt.uint8
 FP8X4 = mybir.dt.float8_e4m3fn_x4
 ALU = mybir.AluOpType
 COPY = mybir.ActivationFunctionType.Copy
+SIGN = mybir.ActivationFunctionType.Sign
 
 P = 128
 PACK = 4
@@ -22,7 +23,8 @@ LAST = PACK - 1
 BANKS = 8
 KIB = 1024
 W1_RAW_AT = 0
-LAST_Y_AT = 8 * KIB
+LAST_Y_AT = 10 * KIB
+LAST_SIGNS_AT = 14 * KIB
 SCALE_ROWS = K // 32
 
 
@@ -128,8 +130,12 @@ def tile_picked_mixscat_none_p_kernel(tc, x_words, x_scales, wa, gt, w1, offs, l
 
         y = {t: keep.tile([P, H], F32, name=f"y{t}", tag=f"y{t}", align_bytes=64) for t in order[:-1]}
         y[LAST] = shared.tile([P, H], F32, name="y_last", offset=LAST_Y_AT, align_bytes=64)
-        a = {t: keep.tile([P, V], F32, name=f"a{t}", tag=f"a{t}", align_bytes=64) for t in order}
-        b = {t: keep.tile([P, V], F32, name=f"b{t}", tag=f"b{t}", align_bytes=64) for t in order}
+        third = order[2]
+        a = {t: keep.tile([P, V], F32, name=f"a{t}", tag=f"a{t}", align_bytes=64)[:] for t in order[:2]}
+        b = {t: keep.tile([P, V], F32, name=f"b{t}", tag=f"b{t}", align_bytes=64)[:] for t in order[:2]}
+        pair = {t: keep.tile([P, 2, V], F32, name=f"pair{t}", tag=f"pair{t}", align_bytes=64) for t in order[2:]}
+        for t in pair:
+            a[t], b[t] = pair[t][:, 0, :], pair[t][:, 1, :]
 
         def project(t, cols, bank, copy):
             acc = psum.tile([P, cols.stop - cols.start], F32, name="acc", tag=f"bank{bank}")
@@ -137,34 +143,53 @@ def tile_picked_mixscat_none_p_kernel(tc, x_words, x_scales, wa, gt, w1, offs, l
             copy(y[t][:, cols], acc[:])
 
         def fetch(values, t, offsets):
-            nc.scalar.activation(values[t][:], y[t][:].indirect(offsets[:]), COPY)
+            nc.scalar.activation(values[t], y[t][:].indirect(offsets[:]), COPY)
 
         project(first, slice(0, HALF), 0, nc.scalar.copy)
+        project(order[1], slice(0, HALF), 3, nc.scalar.copy)
         project(first, slice(HALF, HALF + P), 1, nc.vector.tensor_copy)
         project(first, slice(HALF + P, H), 2, nc.scalar.copy)
-        nc.vector.tensor_copy(a[first][:], y[first][:].indirect(la_sb[:]))
+        nc.vector.tensor_copy(a[first], y[first][:].indirect(la_sb[:]))
         fetch(b, first, lb_sb)
-        for t in order[1:]:
-            project(t, slice(0, H), 2, nc.scalar.copy)
+        for t, following in zip(order[1:], order[2:] + (None,)):
+            halves = [(t, slice(HALF, H))] + ([] if following is None else [(following, slice(0, HALF))])
+            acc = psum.tile([P, 2, HALF], F32, name="acc", tag="bank2")
+            for i, (owner, cols) in enumerate(halves):
+                multiply(nc, acc[:, i, :], x_codes[:, owner, :], x_planes[:, owner, :], wa_codes[:, cols], wa_plane[:, cols])
+            for i, (owner, cols) in enumerate(halves):
+                nc.scalar.copy(y[owner][:, cols], acc[:, i, :])
             fetch(a, t, la_sb)
             fetch(b, t, lb_sb)
 
-        w1_bf = shared.tile([P, N, PACK], BF16, name="w1_bf", offset=LAST_Y_AT + KIB, align_bytes=64)
-        interleave(nc.scalar.copy, w1_bf[:], w1_raw[:])
+        choice = {}
+        for t, signs_at in ((LAST, LAST_SIGNS_AT),):
+            diff = keep.tile([P, V], F32, name=f"diff{t}", tag=f"pair{third}", align_bytes=64)
+            nc.gpsimd.tensor_tensor(diff[:], a[t], b[t], ALU.subtract)
+            signs = shared.tile([P, V], F32, name=f"signs{t}", offset=signs_at, align_bytes=64)
+            nc.scalar.activation(signs[:], diff[:], SIGN)
+            choice[t] = keep.tile([P, 2, V], F32, name=f"choice{t}", tag=f"choice{t}", align_bytes=64)
+            for side, half_sign in enumerate((-0.5, 0.5)):
+                nc.scalar.activation(choice[t][:, side, :], signs[:], COPY, scale=half_sign, bias=0.5)
 
-        zs = {t: keep.tile([P, H], F32, name=f"zs{t}", tag=f"zs{t}", align_bytes=64) for t in order}
+        w1_bf_at = (LAST_SIGNS_AT + KIB // 2, LAST_SIGNS_AT + KIB // 2 - 2 * KIB)
+        w1_bf = [shared.tile([P, HALF, PACK], BF16, name=f"w1_bf{h}", offset=w1_bf_at[h], align_bytes=64) for h in range(2)]
+        for h in range(2):
+            interleave(nc.scalar.copy, w1_bf[h][:], w1_raw[:, :, h * HALF : (h + 1) * HALF])
+
+        second = order[1]
+        zs_tags = {t: f"y{third}" if t == second else f"zs{t}" for t in order}
+        zs = {t: keep.tile([P, H], F32, name=f"zs{t}", tag=zs_tags[t], align_bytes=64) for t in order}
         mn = {t: keep.tile([P, V], F32, name=f"mn{t}", align_bytes=64) for t in order}
-        mx = {t: keep.tile([P, V], F32, name=f"mx{t}", tag=f"y{later}", align_bytes=64) for t, later in zip(order[:2], order[1:])}
-        mx[order[2]] = shared.tile([P, V], F32, name="mx_third", offset=LAST_Y_AT, align_bytes=64)
-        mx[LAST] = shared.tile([P, V], F32, name="mx_last", offset=W1_RAW_AT + 4 * KIB, align_bytes=64)
+        mx = {t: keep.tile([P, V], F32, name=f"mx{t}", align_bytes=64) for t in order[1:3]}
+        mx[first] = keep.tile([P, V], F32, name="mx_first", tag=f"y{second}", align_bytes=64)
         z_both = shared.tile([P, H, PACK], BF16, name="z_both", offset=W1_RAW_AT, align_bytes=64)
         z_bf = [z_both[:, h * HALF : (h + 1) * HALF, :] for h in range(2)]
 
         def take_min(t):
-            nc.vector.tensor_tensor(mn[t][:], a[t][:], b[t][:], ALU.min)
+            nc.vector.tensor_tensor(mn[t][:], a[t], b[t], ALU.min)
 
         def take_max(t):
-            nc.vector.tensor_tensor(mx[t][:], a[t][:], b[t][:], ALU.max)
+            nc.vector.tensor_tensor(mx[t][:], a[t], b[t], ALU.max)
 
         def put_min(t):
             nc.vector.tensor_copy(zs[t][:].indirect(la_sb[:]), mn[t][:])
@@ -177,33 +202,40 @@ def tile_picked_mixscat_none_p_kernel(tc, x_words, x_scales, wa, gt, w1, offs, l
                 nc.scalar.activation(z_bf[h][:, :, t], zs[t][:, h * HALF : (h + 1) * HALF], COPY, scale=gate[:, t : t + 1])
 
         w1_plane = [keep.tile([P, HALF], U8, name=f"w1_plane{h}", align_bytes=64) for h in range(2)]
-        w1_codes = [
-            keep.tile([P, HALF], U32, name="w1_codes0", align_bytes=64),
-            keep.tile([P, HALF], U32, name="w1_codes1", tag=f"a{LAST}", align_bytes=64),
-        ]
 
         def quantize_w1(h):
-            quantize(nc, w1_codes[h][:], w1_plane[h][:], w1_bf[:, h * HALF : (h + 1) * HALF, :])
+            quantize(nc, w1_codes[h][:], w1_plane[h][:], w1_bf[h][:])
 
         take_min(first)
         put_min(first)
-        for earlier, t in zip(order[:2], order[1:3]):
-            take_min(t)
-            take_max(earlier)
-            put_min(t)
-            put_max(earlier)
-            round_z(earlier, range(2))
-            if earlier == first:
-                last_gate = keep.tile([P, 1], F32, name="last_gate", tag=f"zs{first}", align_bytes=64)
-                nc.scalar.copy(last_gate[:], gate[:, LAST:])
-        take_max(order[2])
-        take_min(LAST)
-        put_max(order[2])
+        take_max(first)
+        take_min(second)
+        take_max(second)
+        put_max(first)
+        round_z(first, range(2))
+        last_gate = keep.tile([P, 1], F32, name="last_gate", tag=f"zs{first}", align_bytes=64)
+        nc.scalar.copy(last_gate[:], gate[:, LAST:])
+        take_min(third)
+        take_max(third)
+        put_min(second)
+        put_min(third)
+        put_max(second)
+        round_z(second, range(2))
+        low_last = keep.tile([P, 2, V], F32, name="low_last", tag="last_terms", align_bytes=64)
+        nc.gpsimd.tensor_tensor(low_last[:], pair[LAST][:], choice[LAST][:], ALU.mult)
+        nc.gpsimd.tensor_tensor(mn[LAST][:], low_last[:, 0, :], low_last[:, 1, :], ALU.add)
+        high_last = keep.tile([P, 2, V], F32, name="high_last", tag="last_terms", align_bytes=64)
+        nc.gpsimd.tensor_tensor(high_last[:], pair[LAST][:], choice[LAST][:, ::-1, :], ALU.mult)
+        put_max(third)
+        round_z(third, range(2))
+
+        w1_codes = [
+            keep.tile([P, HALF], U32, name="w1_codes0", tag=f"choice{LAST}", align_bytes=64),
+            shared.tile([P, HALF], U32, name="w1_codes1", offset=w1_bf_at[0], align_bytes=64),
+        ]
         put_min(LAST)
-        round_z(order[2], range(2))
-        take_max(LAST)
         quantize_w1(0)
-        put_max(LAST)
+        nc.vector.tensor_tensor(zs[LAST][:].indirect(lb_sb[:]), high_last[:, 0, :], high_last[:, 1, :], ALU.add)
         quantize_w1(1)
         round_z(LAST, [1])
 

@@ -171,7 +171,7 @@ def tile_picked_mixscat_none_p_kernel(tc, x_words, x_scales, wa, gt, w1, offs, l
             for side, half_sign in enumerate((-0.5, 0.5)):
                 nc.scalar.activation(choice[t][:, side, :], signs[:], COPY, scale=half_sign, bias=0.5)
 
-        w1_bf_at = (LAST_SIGNS_AT + KIB // 2, LAST_SIGNS_AT + KIB // 2 - 2 * KIB)
+        w1_bf_at = (LAST_Y_AT, LAST_SIGNS_AT)
         w1_bf = [shared.tile([P, HALF, PACK], BF16, name=f"w1_bf{h}", offset=w1_bf_at[h], align_bytes=64) for h in range(2)]
         for h in range(2):
             interleave(nc.scalar.copy, w1_bf[h][:], w1_raw[:, :, h * HALF : (h + 1) * HALF])

@@ -224,13 +224,13 @@ def tile_picked_mixscat_none_p_kernel(tc, x_words, x_scales, wa, gt, w1, offs, l
         low_last = keep.tile([P, 2, V], F32, name="low_last", tag="last_terms", align_bytes=64)
         nc.gpsimd.tensor_tensor(low_last[:], pair[LAST][:], choice[LAST][:], ALU.mult)
         nc.gpsimd.tensor_tensor(mn[LAST][:], low_last[:, 0, :], low_last[:, 1, :], ALU.add)
-        high_last = keep.tile([P, 2, V], F32, name="high_last", tag="last_terms", align_bytes=64)
-        nc.gpsimd.tensor_tensor(high_last[:], pair[LAST][:], choice[LAST][:, ::-1, :], ALU.mult)
+        high_last = keep.tile([P, 2, V], F32, name="high_last", align_bytes=64)
+        nc.gpsimd.tensor_tensor(high_last[:], pair[LAST][:], low_last[:], ALU.subtract)
         put_max(third)
         round_z(third, range(2))
 
         w1_codes = [
-            keep.tile([P, HALF], U32, name="w1_codes0", tag=f"choice{LAST}", align_bytes=64),
+            keep.tile([P, HALF], U32, name="w1_codes0", tag="last_terms", align_bytes=64),
             shared.tile([P, HALF], U32, name="w1_codes1", offset=w1_bf_at[0], align_bytes=64),
         ]
         put_min(LAST)

@@ -151,13 +151,18 @@ def tile_picked_mixscat_none_p_kernel(tc, x_words, x_scales, wa, gt, w1, offs, l
         project(first, slice(HALF + P, H), 2, nc.scalar.copy)
         nc.vector.tensor_copy(a[first], y[first][:].indirect(la_sb[:]))
         fetch(b, first, lb_sb)
-        for t, following in zip(order[1:], order[2:] + (None,)):
-            halves = [(t, slice(HALF, H))] + ([] if following is None else [(following, slice(0, HALF))])
-            acc = psum.tile([P, 2, HALF], F32, name="acc", tag="bank2")
-            for i, (owner, cols) in enumerate(halves):
+        second = order[1]
+        project(second, slice(HALF, H), 4, nc.vector.tensor_copy)
+        project(third, slice(0, HALF), 2, nc.vector.tensor_copy)
+        fetch(a, second, la_sb)
+        fetch(b, second, lb_sb)
+        for t, halves in ((third, ((third, 1), (LAST, 0))), (LAST, ((LAST, 1),))):
+            acc = psum.tile([P, 2, HALF], F32, name="acc", tag="bank4")
+            for i, (owner, h) in enumerate(halves):
+                cols = slice(h * HALF, (h + 1) * HALF)
                 multiply(nc, acc[:, i, :], x_codes[:, owner, :], x_planes[:, owner, :], wa_codes[:, cols], wa_plane[:, cols])
-            for i, (owner, cols) in enumerate(halves):
-                nc.scalar.copy(y[owner][:, cols], acc[:, i, :])
+            for i, (owner, h) in enumerate(halves):
+                nc.scalar.copy(y[owner][:, h * HALF : (h + 1) * HALF], acc[:, i, :])
             fetch(a, t, la_sb)
             fetch(b, t, lb_sb)
 
@@ -171,12 +176,16 @@ def tile_picked_mixscat_none_p_kernel(tc, x_words, x_scales, wa, gt, w1, offs, l
             for side, half_sign in enumerate((-0.5, 0.5)):
                 nc.scalar.activation(choice[t][:, side, :], signs[:], COPY, scale=half_sign, bias=0.5)
 
-        w1_bf_at = (LAST_Y_AT, LAST_SIGNS_AT)
-        w1_bf = [shared.tile([P, HALF, PACK], BF16, name=f"w1_bf{h}", offset=w1_bf_at[h], align_bytes=64) for h in range(2)]
-        for h in range(2):
-            interleave(nc.scalar.copy, w1_bf[h][:], w1_raw[:, :, h * HALF : (h + 1) * HALF])
+        w1_pieces = (
+            (slice(0, P), LAST_Y_AT),
+            (slice(P, HALF), LAST_SIGNS_AT - KIB // 2),
+            (slice(HALF, N), LAST_SIGNS_AT + KIB // 2),
+        )
+        w1_bf = []
+        for i, (cols, at) in enumerate(w1_pieces):
+            w1_bf.append(shared.tile([P, cols.stop - cols.start, PACK], BF16, name=f"w1_bf{i}", offset=at, align_bytes=64))
+            interleave(nc.scalar.copy, w1_bf[i][:], w1_raw[:, :, cols])
 
-        second = order[1]
         zs_tags = {t: f"y{third}" if t == second else f"zs{t}" for t in order}
         zs = {t: keep.tile([P, H], F32, name=f"zs{t}", tag=zs_tags[t], align_bytes=64) for t in order}
         mn = {t: keep.tile([P, V], F32, name=f"mn{t}", align_bytes=64) for t in order}
@@ -203,9 +212,6 @@ def tile_picked_mixscat_none_p_kernel(tc, x_words, x_scales, wa, gt, w1, offs, l
 
         w1_plane = [keep.tile([P, HALF], U8, name=f"w1_plane{h}", align_bytes=64) for h in range(2)]
 
-        def quantize_w1(h):
-            quantize(nc, w1_codes[h][:], w1_plane[h][:], w1_bf[h][:])
-
         take_min(first)
         put_min(first)
         take_max(first)
@@ -222,7 +228,8 @@ def tile_picked_mixscat_none_p_kernel(tc, x_words, x_scales, wa, gt, w1, offs, l
         put_max(second)
         round_z(second, range(2))
         low_last = keep.tile([P, 2, V], F32, name="low_last", tag="last_terms", align_bytes=64)
-        nc.gpsimd.tensor_tensor(low_last[:], pair[LAST][:], choice[LAST][:], ALU.mult)
+        for side in range(2):
+            nc.gpsimd.tensor_tensor(low_last[:, side, :], pair[LAST][:, side, :], choice[LAST][:, side, :], ALU.mult)
         nc.gpsimd.tensor_tensor(mn[LAST][:], low_last[:, 0, :], low_last[:, 1, :], ALU.add)
         high_last = keep.tile([P, 2, V], F32, name="high_last", align_bytes=64)
         nc.gpsimd.tensor_tensor(high_last[:], pair[LAST][:], low_last[:], ALU.subtract)
@@ -231,12 +238,13 @@ def tile_picked_mixscat_none_p_kernel(tc, x_words, x_scales, wa, gt, w1, offs, l
 
         w1_codes = [
             keep.tile([P, HALF], U32, name="w1_codes0", tag="last_terms", align_bytes=64),
-            shared.tile([P, HALF], U32, name="w1_codes1", offset=w1_bf_at[0], align_bytes=64),
+            shared.tile([P, HALF], U32, name="w1_codes1", offset=LAST_Y_AT, align_bytes=64),
         ]
         put_min(LAST)
-        quantize_w1(0)
+        for i in range(2):
+            quantize(nc, w1_codes[0][:, w1_pieces[i][0]], w1_plane[0][:, w1_pieces[i][0]], w1_bf[i][:])
         nc.vector.tensor_tensor(zs[LAST][:].indirect(lb_sb[:]), high_last[:, 0, :], high_last[:, 1, :], ALU.add)
-        quantize_w1(1)
+        quantize(nc, w1_codes[1][:], w1_plane[1][:], w1_bf[2][:])
         round_z(LAST, [1])
 
         quarters = (slice(0, P), slice(P, HALF))

@@ -23,8 +23,7 @@ LAST = PACK - 1
 BANKS = 8
 KIB = 1024
 W1_RAW_AT = 0
-LAST_Y_AT = 10 * KIB
-LAST_SIGNS_AT = 14 * KIB
+FOURTH_Y_AT = 8 * KIB
 SCALE_ROWS = K // 32
 
 
@@ -125,80 +124,71 @@ def tile_picked_mixscat_none_p_kernel(tc, x_words, x_scales, wa, gt, w1, offs, l
         gate = keep.tile([P, PACK], F32, name="gate", tag="x_table", align_bytes=64)
         nc.sync.dma_start(gate[:], gt.rearrange("(p t) o -> p (t o)", t=PACK))
 
-        order = (LAST - 1, 0, 1, LAST)
-        first = order[0]
+        first, second, fourth = LAST - 1, 0, 1
+        order = (first, second, LAST, fourth)
 
         y = {t: keep.tile([P, H], F32, name=f"y{t}", tag=f"y{t}", align_bytes=64) for t in order[:-1]}
-        y[LAST] = shared.tile([P, H], F32, name="y_last", offset=LAST_Y_AT, align_bytes=64)
-        third = order[2]
-        a = {t: keep.tile([P, V], F32, name=f"a{t}", tag=f"a{t}", align_bytes=64)[:] for t in order[:2]}
-        b = {t: keep.tile([P, V], F32, name=f"b{t}", tag=f"b{t}", align_bytes=64)[:] for t in order[:2]}
-        pair = {t: keep.tile([P, 2, V], F32, name=f"pair{t}", tag=f"pair{t}", align_bytes=64) for t in order[2:]}
-        for t in pair:
-            a[t], b[t] = pair[t][:, 0, :], pair[t][:, 1, :]
+        y[fourth] = shared.tile([P, H], F32, name="y_fourth", offset=FOURTH_Y_AT, align_bytes=64)
+        a = {t: keep.tile([P, V], F32, name=f"a{t}", tag=f"a{t}", align_bytes=64) for t in order}
+        b = {t: keep.tile([P, V], F32, name=f"b{t}", tag=f"b{t}", align_bytes=64) for t in order}
 
-        def project(t, cols, bank, copy):
-            acc = psum.tile([P, cols.stop - cols.start], F32, name="acc", tag=f"bank{bank}")
-            multiply(nc, acc[:], x_codes[:, t, :], x_planes[:, t, :], wa_codes[:, cols], wa_plane[:, cols])
-            copy(y[t][:, cols], acc[:])
+        def project(bank, copy, pieces):
+            acc = psum.tile([P, len(pieces), pieces[0][1].stop - pieces[0][1].start], F32, name="acc", tag=f"bank{bank}")
+            for i, (t, cols) in enumerate(pieces):
+                multiply(nc, acc[:, i, :], x_codes[:, t, :], x_planes[:, t, :], wa_codes[:, cols], wa_plane[:, cols])
+            for i, (t, cols) in enumerate(pieces):
+                copy(y[t][:, cols], acc[:, i, :])
 
         def fetch(values, t, offsets):
-            nc.scalar.activation(values[t], y[t][:].indirect(offsets[:]), COPY)
+            nc.scalar.activation(values[t][:], y[t][:].indirect(offsets[:]), COPY)
 
-        project(first, slice(0, HALF), 0, nc.scalar.copy)
-        project(order[1], slice(0, HALF), 3, nc.scalar.copy)
-        project(first, slice(HALF, HALF + P), 1, nc.vector.tensor_copy)
-        project(first, slice(HALF + P, H), 2, nc.scalar.copy)
-        nc.vector.tensor_copy(a[first], y[first][:].indirect(la_sb[:]))
+        halves = (slice(0, HALF), slice(HALF, H))
+        project(0, nc.scalar.copy, [(first, halves[0])])
+        project(3, nc.scalar.copy, [(second, halves[0])])
+        project(1, nc.vector.tensor_copy, [(first, slice(HALF, HALF + P))])
+        project(2, nc.scalar.copy, [(first, slice(HALF + P, H))])
+        nc.vector.tensor_copy(a[first][:], y[first][:].indirect(la_sb[:]))
         fetch(b, first, lb_sb)
-        second = order[1]
-        project(second, slice(HALF, H), 4, nc.vector.tensor_copy)
-        project(third, slice(0, HALF), 2, nc.vector.tensor_copy)
+        project(4, nc.vector.tensor_copy, [(second, halves[1])])
+        project(2, nc.vector.tensor_copy, [(LAST, halves[0])])
         fetch(a, second, la_sb)
         fetch(b, second, lb_sb)
-        for t, halves in ((third, ((third, 1), (LAST, 0))), (LAST, ((LAST, 1),))):
-            acc = psum.tile([P, 2, HALF], F32, name="acc", tag="bank4")
-            for i, (owner, h) in enumerate(halves):
-                cols = slice(h * HALF, (h + 1) * HALF)
-                multiply(nc, acc[:, i, :], x_codes[:, owner, :], x_planes[:, owner, :], wa_codes[:, cols], wa_plane[:, cols])
-            for i, (owner, h) in enumerate(halves):
-                nc.scalar.copy(y[owner][:, h * HALF : (h + 1) * HALF], acc[:, i, :])
-            fetch(a, t, la_sb)
-            fetch(b, t, lb_sb)
+        project(4, nc.scalar.copy, [(LAST, halves[1]), (fourth, halves[0])])
+        fetch(a, LAST, la_sb)
+        fetch(b, LAST, lb_sb)
+        project(4, nc.scalar.copy, [(fourth, halves[1])])
+        fetch(a, fourth, la_sb)
+        fetch(b, fourth, lb_sb)
 
-        choice = {}
-        for t, signs_at in ((LAST, LAST_SIGNS_AT),):
-            diff = keep.tile([P, V], F32, name=f"diff{t}", tag=f"pair{third}", align_bytes=64)
-            nc.gpsimd.tensor_tensor(diff[:], a[t], b[t], ALU.subtract)
-            signs = shared.tile([P, V], F32, name=f"signs{t}", offset=signs_at, align_bytes=64)
-            nc.scalar.activation(signs[:], diff[:], SIGN)
-            choice[t] = keep.tile([P, 2, V], F32, name=f"choice{t}", tag=f"choice{t}", align_bytes=64)
-            for side, half_sign in enumerate((-0.5, 0.5)):
-                nc.scalar.activation(choice[t][:, side, :], signs[:], COPY, scale=half_sign, bias=0.5)
+        diff = keep.tile([P, V], F32, name="diff", align_bytes=64)
+        nc.gpsimd.tensor_tensor(diff[:], a[LAST][:], b[LAST][:], ALU.subtract)
+        signs = shared.tile([P, V], F32, name="signs", offset=FOURTH_Y_AT + KIB, align_bytes=64)
+        nc.scalar.activation(signs[:], diff[:], SIGN)
+        weight = []
+        for side, half_sign in enumerate((-0.5, 0.5)):
+            weight.append(keep.tile([P, V], F32, name=f"weight{side}", tag=f"weight{side}", align_bytes=64))
+            nc.scalar.activation(weight[side][:], signs[:], COPY, scale=half_sign, bias=0.5)
 
-        w1_pieces = (
-            (slice(0, P), LAST_Y_AT),
-            (slice(P, HALF), LAST_SIGNS_AT - KIB // 2),
-            (slice(HALF, N), LAST_SIGNS_AT + KIB // 2),
-        )
-        w1_bf = []
-        for i, (cols, at) in enumerate(w1_pieces):
-            w1_bf.append(shared.tile([P, cols.stop - cols.start, PACK], BF16, name=f"w1_bf{i}", offset=at, align_bytes=64))
-            interleave(nc.scalar.copy, w1_bf[i][:], w1_raw[:, :, cols])
+        w1_bf = shared.tile([P, N, PACK], BF16, name="w1_bf", offset=FOURTH_Y_AT + KIB, align_bytes=64)
+        for cols in halves:
+            interleave(nc.scalar.copy, w1_bf[:, cols, :], w1_raw[:, :, cols])
 
-        zs_tags = {t: f"y{third}" if t == second else f"zs{t}" for t in order}
-        zs = {t: keep.tile([P, H], F32, name=f"zs{t}", tag=zs_tags[t], align_bytes=64) for t in order}
-        mn = {t: keep.tile([P, V], F32, name=f"mn{t}", align_bytes=64) for t in order}
-        mx = {t: keep.tile([P, V], F32, name=f"mx{t}", align_bytes=64) for t in order[1:3]}
-        mx[first] = keep.tile([P, V], F32, name="mx_first", tag=f"y{second}", align_bytes=64)
+        zs = {t: keep.tile([P, H], F32, name=f"zs{t}", tag=f"zs{t}", align_bytes=64) for t in order[:-1]}
+        zs[fourth] = keep.tile([P, H], F32, name="zs_fourth", tag="weight0", align_bytes=64)
+        mn = {t: keep.tile([P, V], F32, name=f"mn{t}", align_bytes=64) for t in (first, second, fourth)}
+        mx = {
+            first: keep.tile([P, V], F32, name="mx_first", tag=f"y{second}", align_bytes=64),
+            second: shared.tile([P, V], F32, name="mx_second", offset=FOURTH_Y_AT, align_bytes=64),
+            fourth: keep.tile([P, V], F32, name="mx_fourth", tag="mx_fourth", align_bytes=64),
+        }
         z_both = shared.tile([P, H, PACK], BF16, name="z_both", offset=W1_RAW_AT, align_bytes=64)
-        z_bf = [z_both[:, h * HALF : (h + 1) * HALF, :] for h in range(2)]
+        z_bf = [z_both[:, cols, :] for cols in halves]
 
         def take_min(t):
-            nc.vector.tensor_tensor(mn[t][:], a[t], b[t], ALU.min)
+            nc.vector.tensor_tensor(mn[t][:], a[t][:], b[t][:], ALU.min)
 
         def take_max(t):
-            nc.vector.tensor_tensor(mx[t][:], a[t], b[t], ALU.max)
+            nc.vector.tensor_tensor(mx[t][:], a[t][:], b[t][:], ALU.max)
 
         def put_min(t):
             nc.vector.tensor_copy(zs[t][:].indirect(la_sb[:]), mn[t][:])
@@ -206,45 +196,43 @@ def tile_picked_mixscat_none_p_kernel(tc, x_words, x_scales, wa, gt, w1, offs, l
         def put_max(t):
             nc.vector.tensor_copy(zs[t][:].indirect(lb_sb[:]), mx[t][:])
 
-        def round_z(t, halves):
-            for h in halves:
-                nc.scalar.activation(z_bf[h][:, :, t], zs[t][:, h * HALF : (h + 1) * HALF], COPY, scale=gate[:, t : t + 1])
-
-        w1_plane = [keep.tile([P, HALF], U8, name=f"w1_plane{h}", align_bytes=64) for h in range(2)]
+        def round_z(t, which):
+            for h in which:
+                nc.scalar.activation(z_bf[h][:, :, t], zs[t][:, halves[h]], COPY, scale=gate[:, t : t + 1])
 
         take_min(first)
         put_min(first)
         take_max(first)
         take_min(second)
-        take_max(second)
         put_max(first)
+        put_min(second)
         round_z(first, range(2))
         last_gate = keep.tile([P, 1], F32, name="last_gate", tag=f"zs{first}", align_bytes=64)
         nc.scalar.copy(last_gate[:], gate[:, LAST:])
-        take_min(third)
-        take_max(third)
-        put_min(second)
-        put_min(third)
+        take_max(second)
+        take_min(fourth)
+        take_max(fourth)
         put_max(second)
         round_z(second, range(2))
-        low_last = keep.tile([P, 2, V], F32, name="low_last", tag="last_terms", align_bytes=64)
-        for side in range(2):
-            nc.gpsimd.tensor_tensor(low_last[:, side, :], pair[LAST][:, side, :], choice[LAST][:, side, :], ALU.mult)
-        nc.gpsimd.tensor_tensor(mn[LAST][:], low_last[:, 0, :], low_last[:, 1, :], ALU.add)
-        high_last = keep.tile([P, 2, V], F32, name="high_last", align_bytes=64)
-        nc.gpsimd.tensor_tensor(high_last[:], pair[LAST][:], low_last[:], ALU.subtract)
-        put_max(third)
-        round_z(third, range(2))
 
-        w1_codes = [
-            keep.tile([P, HALF], U32, name="w1_codes0", tag="last_terms", align_bytes=64),
-            shared.tile([P, HALF], U32, name="w1_codes1", offset=LAST_Y_AT, align_bytes=64),
-        ]
-        put_min(LAST)
-        for i in range(2):
-            quantize(nc, w1_codes[0][:, w1_pieces[i][0]], w1_plane[0][:, w1_pieces[i][0]], w1_bf[i][:])
-        nc.vector.tensor_tensor(zs[LAST][:].indirect(lb_sb[:]), high_last[:, 0, :], high_last[:, 1, :], ALU.add)
-        quantize(nc, w1_codes[1][:], w1_plane[1][:], w1_bf[2][:])
+        low, high = [], []
+        for side, values in enumerate((a, b)):
+            low.append(keep.tile([P, V], F32, name=f"low{side}", tag=f"{'ab'[side]}{fourth}", align_bytes=64))
+            nc.gpsimd.tensor_tensor(low[side][:], values[LAST][:], weight[side][:], ALU.mult)
+        for side, values in enumerate((a, b)):
+            high.append(keep.tile([P, V], F32, name=f"high{side}", align_bytes=64))
+            nc.gpsimd.tensor_tensor(high[side][:], values[LAST][:], low[side][:], ALU.subtract)
+
+        put_min(fourth)
+        nc.vector.tensor_tensor(zs[LAST][:].indirect(la_sb[:]), low[0][:], low[1][:], ALU.add)
+        put_max(fourth)
+        round_z(fourth, range(2))
+        nc.vector.tensor_tensor(zs[LAST][:].indirect(lb_sb[:]), high[0][:], high[1][:], ALU.add)
+
+        w1_codes = keep.tile([P, N], U32, name="w1_codes", tag="mx_fourth", align_bytes=64)
+        w1_plane = keep.tile([P, N], U8, name="w1_plane", align_bytes=64)
+        for cols in halves:
+            quantize(nc, w1_codes[:, cols], w1_plane[:, cols], w1_bf[:, cols, :])
         round_z(LAST, [1])
 
         quarters = (slice(0, P), slice(P, HALF))
@@ -258,8 +246,8 @@ def tile_picked_mixscat_none_p_kernel(tc, x_words, x_scales, wa, gt, w1, offs, l
         quantize(nc, z_codes[1][:], z_plane[1][:], z_bf[1])
 
         def mix(acc, h, m, cols):
-            places = slice(m % 2 * P, (m % 2 + 1) * P)
-            multiply(nc, acc, w1_codes[m // 2][:, places], w1_plane[m // 2][:, places], z_codes[h][:, cols], z_plane[h][:, cols])
+            places = slice(m * P, (m + 1) * P)
+            multiply(nc, acc, w1_codes[:, places], w1_plane[:, places], z_codes[h][:, cols], z_plane[h][:, cols])
 
         copies = (nc.scalar.copy, nc.vector.tensor_copy)
         banks = list(range(BANKS)) + [0]

@@ -24,6 +24,7 @@ BANKS = 8
 KIB = 1024
 W1_RAW_AT = 0
 FOURTH_Y_AT = 8 * KIB
+SECOND_PAIR_AT = (14 * KIB, 16 * KIB)
 SCALE_ROWS = K // 32
 
 
@@ -129,8 +130,11 @@ def tile_picked_mixscat_none_p_kernel(tc, x_words, x_scales, wa, gt, w1, offs, l
 
         y = {t: keep.tile([P, H], F32, name=f"y{t}", tag=f"y{t}", align_bytes=64) for t in order[:-1]}
         y[fourth] = shared.tile([P, H], F32, name="y_fourth", offset=FOURTH_Y_AT, align_bytes=64)
-        a = {t: keep.tile([P, V], F32, name=f"a{t}", tag=f"a{t}", align_bytes=64) for t in order}
-        b = {t: keep.tile([P, V], F32, name=f"b{t}", tag=f"b{t}", align_bytes=64) for t in order}
+        a = {t: keep.tile([P, V], F32, name=f"a{t}", align_bytes=64) for t in (first, LAST)}
+        b = {t: keep.tile([P, V], F32, name=f"b{t}", align_bytes=64) for t in (first, LAST, fourth)}
+        a[fourth] = keep.tile([P, V], F32, name="a_fourth", tag="a_fourth", align_bytes=64)
+        a[second] = shared.tile([P, V], F32, name="a_second", offset=SECOND_PAIR_AT[0], align_bytes=64)
+        b[second] = shared.tile([P, V], F32, name="b_second", offset=SECOND_PAIR_AT[1], align_bytes=64)
 
         def project(bank, copy, pieces):
             acc = psum.tile([P, len(pieces), pieces[0][1].stop - pieces[0][1].start], F32, name="acc", tag=f"bank{bank}")
@@ -173,13 +177,11 @@ def tile_picked_mixscat_none_p_kernel(tc, x_words, x_scales, wa, gt, w1, offs, l
         for cols in halves:
             interleave(nc.scalar.copy, w1_bf[:, cols, :], w1_raw[:, :, cols])
 
-        zs = {t: keep.tile([P, H], F32, name=f"zs{t}", tag=f"zs{t}", align_bytes=64) for t in order[:-1]}
-        zs[fourth] = keep.tile([P, H], F32, name="zs_fourth", tag="weight0", align_bytes=64)
+        zs = {t: keep.tile([P, H], F32, name=f"zs{t}", tag=f"zs{t}", align_bytes=64) for t in order}
         mn = {t: keep.tile([P, V], F32, name=f"mn{t}", align_bytes=64) for t in (first, second, fourth)}
         mx = {
             first: keep.tile([P, V], F32, name="mx_first", tag=f"y{second}", align_bytes=64),
             second: shared.tile([P, V], F32, name="mx_second", offset=FOURTH_Y_AT, align_bytes=64),
-            fourth: keep.tile([P, V], F32, name="mx_fourth", tag="mx_fourth", align_bytes=64),
         }
         z_both = shared.tile([P, H, PACK], BF16, name="z_both", offset=W1_RAW_AT, align_bytes=64)
         z_bf = [z_both[:, cols, :] for cols in halves]
@@ -211,28 +213,41 @@ def tile_picked_mixscat_none_p_kernel(tc, x_words, x_scales, wa, gt, w1, offs, l
         nc.scalar.copy(last_gate[:], gate[:, LAST:])
         take_max(second)
         take_min(fourth)
-        take_max(fourth)
         put_max(second)
         round_z(second, range(2))
-
-        low, high = [], []
-        for side, values in enumerate((a, b)):
-            low.append(keep.tile([P, V], F32, name=f"low{side}", tag=f"{'ab'[side]}{fourth}", align_bytes=64))
-            nc.gpsimd.tensor_tensor(low[side][:], values[LAST][:], weight[side][:], ALU.mult)
-        for side, values in enumerate((a, b)):
-            high.append(keep.tile([P, V], F32, name=f"high{side}", align_bytes=64))
-            nc.gpsimd.tensor_tensor(high[side][:], values[LAST][:], low[side][:], ALU.subtract)
-
         put_min(fourth)
-        nc.vector.tensor_tensor(zs[LAST][:].indirect(la_sb[:]), low[0][:], low[1][:], ALU.add)
+
+        low = []
+        for side, values in enumerate((a, b)):
+            low.append(shared.tile([P, V], F32, name=f"low{side}", offset=SECOND_PAIR_AT[side], align_bytes=64))
+            nc.gpsimd.tensor_tensor(low[side][:], values[LAST][:], weight[side][:], ALU.mult)
+        high_a = shared.tile([P, V], F32, name="high_a", offset=SECOND_PAIR_AT[0] + KIB, align_bytes=64)
+        nc.gpsimd.tensor_tensor(high_a[:], a[LAST][:], low[0][:], ALU.subtract)
+        mn[LAST] = keep.tile([P, V], F32, name="mn_last", align_bytes=64)
+        nc.gpsimd.tensor_tensor(mn[LAST][:], low[0][:], low[1][:], ALU.add)
+
+        mx[fourth] = shared.tile([P, V], F32, name="mx_fourth", offset=SECOND_PAIR_AT[0], align_bytes=64)
+        take_max(fourth)
+        high_b = keep.tile([P, V], F32, name="high_b", tag="a_fourth", align_bytes=64)
+        nc.gpsimd.tensor_tensor(high_b[:], b[LAST][:], low[1][:], ALU.subtract)
+        mx[LAST] = keep.tile([P, V], F32, name="mx_last", align_bytes=64)
+        nc.gpsimd.tensor_tensor(mx[LAST][:], high_a[:], high_b[:], ALU.add)
+
+        put_min(LAST)
         put_max(fourth)
         round_z(fourth, range(2))
-        nc.vector.tensor_tensor(zs[LAST][:].indirect(lb_sb[:]), high[0][:], high[1][:], ALU.add)
+        put_max(LAST)
 
-        w1_codes = keep.tile([P, N], U32, name="w1_codes", tag="mx_fourth", align_bytes=64)
-        w1_plane = keep.tile([P, N], U8, name="w1_plane", align_bytes=64)
-        for cols in halves:
-            quantize(nc, w1_codes[:, cols], w1_plane[:, cols], w1_bf[:, cols, :])
+        w1_codes = [
+            shared.tile([P, HALF], U32, name="w1_codes0", offset=SECOND_PAIR_AT[0] + KIB // 2, align_bytes=64),
+            keep.tile([P, HALF], U32, name="w1_codes1", tag=f"zs{first}", align_bytes=64),
+        ]
+        w1_plane = [keep.tile([P, HALF], U8, name=f"w1_plane{h}", align_bytes=64) for h in range(2)]
+
+        def quantize_w1(h):
+            quantize(nc, w1_codes[h][:], w1_plane[h][:], w1_bf[:, halves[h], :])
+
+        quantize_w1(0)
         round_z(LAST, [1])
 
         quarters = (slice(0, P), slice(P, HALF))
@@ -243,11 +258,12 @@ def tile_picked_mixscat_none_p_kernel(tc, x_words, x_scales, wa, gt, w1, offs, l
         z_plane = [keep.tile([P, HALF], U8, name=f"z_plane{h}", align_bytes=64) for h in range(2)]
         for cols in quarters:
             quantize(nc, z_codes[0][:, cols], z_plane[0][:, cols], z_bf[0][:, cols, :])
+        quantize_w1(1)
         quantize(nc, z_codes[1][:], z_plane[1][:], z_bf[1])
 
         def mix(acc, h, m, cols):
-            places = slice(m * P, (m + 1) * P)
-            multiply(nc, acc, w1_codes[:, places], w1_plane[:, places], z_codes[h][:, cols], z_plane[h][:, cols])
+            places = slice(m % 2 * P, (m % 2 + 1) * P)
+            multiply(nc, acc, w1_codes[m // 2][:, places], w1_plane[m // 2][:, places], z_codes[h][:, cols], z_plane[h][:, cols])
 
         copies = (nc.scalar.copy, nc.vector.tensor_copy)
         banks = list(range(BANKS)) + [0]

@@ -24,7 +24,10 @@ BANKS = 8
 KIB = 1024
 W1_RAW_AT = 0
 FOURTH_Y_AT = 8 * KIB
-SECOND_PAIR_AT = (14 * KIB, 16 * KIB)
+SIGNS_AT = 10 * KIB
+WEIGHTS_AT = (18 * KIB, 20 * KIB)
+SECOND_PAIR_AT = (19 * KIB, 16 * KIB)
+FOURTH_PAIR_AT = (15 * KIB, 17 * KIB)
 SCALE_ROWS = K // 32
 
 
@@ -131,8 +134,9 @@ def tile_picked_mixscat_none_p_kernel(tc, x_words, x_scales, wa, gt, w1, offs, l
         y = {t: keep.tile([P, H], F32, name=f"y{t}", tag=f"y{t}", align_bytes=64) for t in order[:-1]}
         y[fourth] = shared.tile([P, H], F32, name="y_fourth", offset=FOURTH_Y_AT, align_bytes=64)
         a = {t: keep.tile([P, V], F32, name=f"a{t}", align_bytes=64) for t in (first, LAST)}
-        b = {t: keep.tile([P, V], F32, name=f"b{t}", align_bytes=64) for t in (first, LAST, fourth)}
-        a[fourth] = keep.tile([P, V], F32, name="a_fourth", tag="a_fourth", align_bytes=64)
+        b = {t: keep.tile([P, V], F32, name=f"b{t}", align_bytes=64) for t in (first, LAST)}
+        a[fourth] = shared.tile([P, V], F32, name="a_fourth", offset=FOURTH_PAIR_AT[0], align_bytes=64)
+        b[fourth] = shared.tile([P, V], F32, name="b_fourth", offset=FOURTH_PAIR_AT[1], align_bytes=64)
         a[second] = shared.tile([P, V], F32, name="a_second", offset=SECOND_PAIR_AT[0], align_bytes=64)
         b[second] = shared.tile([P, V], F32, name="b_second", offset=SECOND_PAIR_AT[1], align_bytes=64)
 
@@ -166,14 +170,14 @@ def tile_picked_mixscat_none_p_kernel(tc, x_words, x_scales, wa, gt, w1, offs, l
 
         diff = keep.tile([P, V], F32, name="diff", align_bytes=64)
         nc.gpsimd.tensor_tensor(diff[:], a[LAST][:], b[LAST][:], ALU.subtract)
-        signs = shared.tile([P, V], F32, name="signs", offset=FOURTH_Y_AT + KIB, align_bytes=64)
+        signs = shared.tile([P, V], F32, name="signs", offset=SIGNS_AT, align_bytes=64)
         nc.scalar.activation(signs[:], diff[:], SIGN)
         weight = []
         for side, half_sign in enumerate((-0.5, 0.5)):
-            weight.append(keep.tile([P, V], F32, name=f"weight{side}", tag=f"weight{side}", align_bytes=64))
+            weight.append(shared.tile([P, V], F32, name=f"weight{side}", offset=WEIGHTS_AT[side], align_bytes=64))
             nc.scalar.activation(weight[side][:], signs[:], COPY, scale=half_sign, bias=0.5)
 
-        w1_bf = shared.tile([P, N, PACK], BF16, name="w1_bf", offset=FOURTH_Y_AT + KIB, align_bytes=64)
+        w1_bf = shared.tile([P, N, PACK], BF16, name="w1_bf", offset=SIGNS_AT, align_bytes=64)
         for cols in halves:
             interleave(nc.scalar.copy, w1_bf[:, cols, :], w1_raw[:, :, cols])
 
@@ -221,25 +225,23 @@ def tile_picked_mixscat_none_p_kernel(tc, x_words, x_scales, wa, gt, w1, offs, l
         for side, values in enumerate((a, b)):
             low.append(shared.tile([P, V], F32, name=f"low{side}", offset=SECOND_PAIR_AT[side], align_bytes=64))
             nc.gpsimd.tensor_tensor(low[side][:], values[LAST][:], weight[side][:], ALU.mult)
-        high_a = shared.tile([P, V], F32, name="high_a", offset=SECOND_PAIR_AT[0] + KIB, align_bytes=64)
-        nc.gpsimd.tensor_tensor(high_a[:], a[LAST][:], low[0][:], ALU.subtract)
         mn[LAST] = keep.tile([P, V], F32, name="mn_last", align_bytes=64)
         nc.gpsimd.tensor_tensor(mn[LAST][:], low[0][:], low[1][:], ALU.add)
 
         mx[fourth] = shared.tile([P, V], F32, name="mx_fourth", offset=SECOND_PAIR_AT[0], align_bytes=64)
         take_max(fourth)
-        high_b = keep.tile([P, V], F32, name="high_b", tag="a_fourth", align_bytes=64)
-        nc.gpsimd.tensor_tensor(high_b[:], b[LAST][:], low[1][:], ALU.subtract)
-        mx[LAST] = keep.tile([P, V], F32, name="mx_last", align_bytes=64)
-        nc.gpsimd.tensor_tensor(mx[LAST][:], high_a[:], high_b[:], ALU.add)
+        high = []
+        for side, values in enumerate((a, b)):
+            high.append(shared.tile([P, V], F32, name=f"high{side}", offset=FOURTH_PAIR_AT[side], align_bytes=64))
+            nc.gpsimd.tensor_tensor(high[side][:], values[LAST][:], weight[1 - side][:], ALU.mult)
 
         put_min(LAST)
         put_max(fourth)
         round_z(fourth, range(2))
-        put_max(LAST)
+        nc.vector.tensor_tensor(zs[LAST][:].indirect(lb_sb[:]), high[0][:], high[1][:], ALU.add)
 
         w1_codes = [
-            shared.tile([P, HALF], U32, name="w1_codes0", offset=SECOND_PAIR_AT[0] + KIB // 2, align_bytes=64),
+            shared.tile([P, HALF], U32, name="w1_codes0", offset=SECOND_PAIR_AT[0] - KIB // 2, align_bytes=64),
             keep.tile([P, HALF], U32, name="w1_codes1", tag=f"zs{first}", align_bytes=64),
         ]
         w1_plane = [keep.tile([P, HALF], U8, name=f"w1_plane{h}", align_bytes=64) for h in range(2)]

from contextlib import ExitStack

import concourse.mybir as mybir

K, T, S, V, N, H = 512, 2048, 512, 256, 512, 512
FLOPS = 2 * K * S * H + 2 * S * N * H

F32 = mybir.dt.float32
BF16 = mybir.dt.bfloat16
I32 = mybir.dt.int32
U32 = mybir.dt.uint32
U16 = mybir.dt.uint16
U8 = mybir.dt.uint8
FP8X4 = mybir.dt.float8_e4m3fn_x4
ALU = mybir.AluOpType
COPY = mybir.ActivationFunctionType.Copy
SIGN = mybir.ActivationFunctionType.Sign

P = 128
PACK = 4
HALF = 256
LAST = PACK - 1
BANKS = 8
KIB = 1024
W1_RAW_AT = 0
FOURTH_Y_AT = 8 * KIB
SIGNS_AT = 10 * KIB
WEIGHTS_AT = (18 * KIB, 20 * KIB)
SECOND_PAIR_AT = (19 * KIB, 16 * KIB)
FOURTH_PAIR_AT = (15 * KIB, 17 * KIB)
SCALE_ROWS = K // 32


def interleave(copy, grouped, raw):
    copy(
        out=grouped.rearrange("p (c i) j -> p c j i", i=4),
        in_=raw.rearrange("p j (c i) -> p c j i", i=4),
    )


def quantize(nc, codes, plane, grouped):
    nc.vector.quantize_mx(out=codes.bitcast(FP8X4), scales=plane, in_=grouped.rearrange("p n j -> p (n j)"))


def multiply(nc, acc, still_codes, still_plane, moving_codes, moving_plane):
    nc.tensor.matmul_mx(
        out=acc,
        lhsT=still_codes.bitcast(FP8X4),
        lhsT_scale=still_plane,
        rhs=moving_codes.bitcast(FP8X4),
        rhs_scale=moving_plane,
        start=True,
        stop=True,
    )


def tile_picked_mixscat_none_p_kernel(tc, x_words, x_scales, wa, gt, w1, offs, la, lb, out):
    nc = tc.nc
    with ExitStack() as ctx:
        keep = ctx.enter_context(tc.tile_pool(name="keep", bufs=1))
        shared = ctx.enter_context(tc.tile_pool(name="shared", bufs=1))
        psum = ctx.enter_context(tc.psum_pool(name="psum", bufs=1))

        offs_sb = keep.tile([P, S // 16], U16, name="offs_sb")
        la_sb = keep.tile([P, V // 16], U16, name="la_sb")
        lb_sb = keep.tile([P, V // 16], U16, name="lb_sb")
        x_table = keep.tile([P, T], I32, name="x_table", tag="x_table", align_bytes=64)
        s_table = keep.tile([P, T], U8, name="s_table", align_bytes=64)
        wa_first = keep.tile([P, 2, H], F32, name="wa_first", align_bytes=64)
        wa_second = [
            keep.tile([P, 2, HALF], F32, name="wa_second0", align_bytes=64),
            shared.tile([P, 2, HALF], F32, name="wa_second1", offset=W1_RAW_AT, align_bytes=64),
        ]

        nc.sync.dma_start(offs_sb[:], offs)
        nc.scalar.dma_start(s_table[P - SCALE_ROWS :, :].bitcast(I32), x_scales[0].bitcast(I32))
        nc.sync.dma_start(x_table[:], x_words[0].rearrange("p n r -> p (n r)").bitcast(I32))
        wa_rows = wa.rearrange("(p j) n -> p j n", j=PACK)
        nc.sync.dma_start(wa_first[:], wa_rows[:, :2, :])
        for h in range(2):
            nc.sync.dma_start(wa_second[h][:], wa_rows[:, 2:, h * HALF : (h + 1) * HALF])
        nc.sync.dma_start(la_sb[:], la)
        nc.sync.dma_start(lb_sb[:], lb)

        warm = keep.tile([P, 2], F32, name="warm", align_bytes=64)
        nc.vector.memset(warm[:, :1], 0.0)
        nc.scalar.copy(warm[:, 1:], warm[:, :1])

        nc.vector.memset(s_table[: P - SCALE_ROWS, :].bitcast(I32), 0)
        s_picked = keep.tile([P, S], U8, name="s_picked", align_bytes=64)
        nc.vector.tensor_copy(s_picked[:], s_table[:].indirect(offs_sb[:]))
        x_planes = keep.tile([P, PACK, P], U8, name="x_planes", align_bytes=64)
        nc.vector.tensor_copy(x_planes[:], s_picked[:].rearrange("p (m t) -> p t m", t=PACK))
        plane_words = x_planes[:].rearrange("p t m -> p (t m)").bitcast(I32)
        for q in range(4):
            first = P - SCALE_ROWS + 4 * q
            nc.scalar.dma_start(plane_words[32 * q : 32 * q + 4, :], plane_words[first : first + 4, :])
        x_codes = keep.tile([P, PACK, P], U32, name="x_codes", align_bytes=64)
        nc.vector.tensor_copy(x_codes[:].rearrange("p t m -> p m t"), x_table[:].bitcast(U32).indirect(offs_sb[:]))

        wa_codes = keep.tile([P, H], U32, name="wa_codes", align_bytes=64)
        wa_plane = keep.tile([P, H], U8, name="wa_plane", align_bytes=64)
        wa_bf = [keep.tile([P, P, PACK], BF16, name=f"wa_bf{q}", align_bytes=64) for q in range(4)]

        def round_first(copy, q):
            interleave(copy, wa_bf[q][:, :, :2], wa_first[:, :, q * P : (q + 1) * P])

        def round_second(copy, q):
            interleave(copy, wa_bf[q][:, :, 2:], wa_second[q // 2][:, :, q % 2 * P : (q % 2 + 1) * P])

        def quantize_wa(q):
            quantize(nc, wa_codes[:, q * P : (q + 1) * P], wa_plane[:, q * P : (q + 1) * P], wa_bf[q][:])

        for q in range(3):
            round_first(nc.scalar.copy, q)
        round_first(nc.vector.tensor_copy, 3)
        for q in range(2):
            round_second(nc.vector.tensor_copy, q)
        for q in range(2):
            quantize_wa(q)
        round_second(nc.scalar.copy, 2)
        round_second(nc.vector.tensor_copy, 3)
        for q in range(2, 4):
            quantize_wa(q)

        w1_raw = shared.tile([P, PACK, N], F32, name="w1_raw", offset=W1_RAW_AT, align_bytes=64)
        nc.sync.dma_start(w1_raw[:], w1.rearrange("(p j) n -> p j n", j=PACK))
        gate = keep.tile([P, PACK], F32, name="gate", tag="x_table", align_bytes=64)
        nc.sync.dma_start(gate[:], gt.rearrange("(p t) o -> p (t o)", t=PACK))

        first, second, fourth = LAST - 1, 0, 1
        order = (first, second, LAST, fourth)

        y = {t: keep.tile([P, H], F32, name=f"y{t}", tag=f"y{t}", align_bytes=64) for t in order[:-1]}
        y[fourth] = shared.tile([P, H], F32, name="y_fourth", offset=FOURTH_Y_AT, align_bytes=64)
        a = {t: keep.tile([P, V], F32, name=f"a{t}", align_bytes=64) for t in (first, LAST)}
        b = {t: keep.tile([P, V], F32, name=f"b{t}", align_bytes=64) for t in (first, LAST)}
        a[fourth] = shared.tile([P, V], F32, name="a_fourth", offset=FOURTH_PAIR_AT[0], align_bytes=64)
        b[fourth] = shared.tile([P, V], F32, name="b_fourth", offset=FOURTH_PAIR_AT[1], align_bytes=64)
        a[second] = shared.tile([P, V], F32, name="a_second", offset=SECOND_PAIR_AT[0], align_bytes=64)
        b[second] = shared.tile([P, V], F32, name="b_second", offset=SECOND_PAIR_AT[1], align_bytes=64)

        def project(bank, copy, pieces):
            acc = psum.tile([P, len(pieces), pieces[0][1].stop - pieces[0][1].start], F32, name="acc", tag=f"bank{bank}")
            for i, (t, cols) in enumerate(pieces):
                multiply(nc, acc[:, i, :], x_codes[:, t, :], x_planes[:, t, :], wa_codes[:, cols], wa_plane[:, cols])
            for i, (t, cols) in enumerate(pieces):
                copy(y[t][:, cols], acc[:, i, :])

        def fetch(values, t, offsets):
            nc.scalar.activation(values[t][:], y[t][:].indirect(offsets[:]), COPY)

        halves = (slice(0, HALF), slice(HALF, H))
        project(0, nc.scalar.copy, [(first, halves[0])])
        project(3, nc.scalar.copy, [(second, halves[0])])
        project(1, nc.vector.tensor_copy, [(first, slice(HALF, HALF + P))])
        project(2, nc.scalar.copy, [(first, slice(HALF + P, H))])
        nc.vector.tensor_copy(a[first][:], y[first][:].indirect(la_sb[:]))
        fetch(b, first, lb_sb)
        project(4, nc.vector.tensor_copy, [(second, halves[1])])
        project(2, nc.vector.tensor_copy, [(LAST, halves[0])])
        fetch(a, second, la_sb)
        fetch(b, second, lb_sb)
        project(4, nc.scalar.copy, [(LAST, halves[1]), (fourth, halves[0])])
        fetch(a, LAST, la_sb)
        fetch(b, LAST, lb_sb)
        project(4, nc.scalar.copy, [(fourth, halves[1])])
        fetch(a, fourth, la_sb)
        fetch(b, fourth, lb_sb)

        diff = keep.tile([P, V], F32, name="diff", align_bytes=64)
        nc.gpsimd.tensor_tensor(diff[:], a[LAST][:], b[LAST][:], ALU.subtract)
        signs = shared.tile([P, V], F32, name="signs", offset=SIGNS_AT, align_bytes=64)
        nc.scalar.activation(signs[:], diff[:], SIGN)
        weight = []
        for side, half_sign in enumerate((-0.5, 0.5)):
            weight.append(shared.tile([P, V], F32, name=f"weight{side}", offset=WEIGHTS_AT[side], align_bytes=64))
            nc.scalar.activation(weight[side][:], signs[:], COPY, scale=half_sign, bias=0.5)

        w1_bf = shared.tile([P, N, PACK], BF16, name="w1_bf", offset=SIGNS_AT, align_bytes=64)
        for cols in halves:
            interleave(nc.scalar.copy, w1_bf[:, cols, :], w1_raw[:, :, cols])

        zs = {t: keep.tile([P, H], F32, name=f"zs{t}", tag=f"zs{t}", align_bytes=64) for t in order}
        mn = {t: keep.tile([P, V], F32, name=f"mn{t}", align_bytes=64) for t in (first, second, fourth)}
        mx = {
            first: keep.tile([P, V], F32, name="mx_first", tag=f"y{second}", align_bytes=64),
            second: shared.tile([P, V], F32, name="mx_second", offset=FOURTH_Y_AT, align_bytes=64),
        }
        z_both = shared.tile([P, H, PACK], BF16, name="z_both", offset=W1_RAW_AT, align_bytes=64)
        z_bf = [z_both[:, cols, :] for cols in halves]

        def take_min(t):
            nc.vector.tensor_tensor(mn[t][:], a[t][:], b[t][:], ALU.min)

        def take_max(t):
            nc.vector.tensor_tensor(mx[t][:], a[t][:], b[t][:], ALU.max)

        def put_min(t):
            nc.vector.tensor_copy(zs[t][:].indirect(la_sb[:]), mn[t][:])

        def put_max(t):
            nc.vector.tensor_copy(zs[t][:].indirect(lb_sb[:]), mx[t][:])

        def round_z(t, which):
            for h in which:
                nc.scalar.activation(z_bf[h][:, :, t], zs[t][:, halves[h]], COPY, scale=gate[:, t : t + 1])

        take_min(first)
        put_min(first)
        take_max(first)
        take_min(second)
        put_max(first)
        put_min(second)
        round_z(first, range(2))
        last_gate = keep.tile([P, 1], F32, name="last_gate", tag=f"zs{first}", align_bytes=64)
        nc.scalar.copy(last_gate[:], gate[:, LAST:])
        take_max(second)
        take_min(fourth)
        put_max(second)
        round_z(second, range(2))
        put_min(fourth)

        low = []
        for side, values in enumerate((a, b)):
            low.append(shared.tile([P, V], F32, name=f"low{side}", offset=SECOND_PAIR_AT[side], align_bytes=64))
            nc.gpsimd.tensor_tensor(low[side][:], values[LAST][:], weight[side][:], ALU.mult)
        mn[LAST] = keep.tile([P, V], F32, name="mn_last", align_bytes=64)
        nc.gpsimd.tensor_tensor(mn[LAST][:], low[0][:], low[1][:], ALU.add)

        mx[fourth] = shared.tile([P, V], F32, name="mx_fourth", offset=SECOND_PAIR_AT[0], align_bytes=64)
        take_max(fourth)
        high = []
        for side, values in enumerate((a, b)):
            high.append(shared.tile([P, V], F32, name=f"high{side}", offset=FOURTH_PAIR_AT[side], align_bytes=64))
            nc.gpsimd.tensor_tensor(high[side][:], values[LAST][:], weight[1 - side][:], ALU.mult)

        put_min(LAST)
        put_max(fourth)
        round_z(fourth, range(2))
        nc.vector.tensor_tensor(zs[LAST][:].indirect(lb_sb[:]), high[0][:], high[1][:], ALU.add)

        w1_codes = [
            shared.tile([P, HALF], U32, name="w1_codes0", offset=SECOND_PAIR_AT[0] - KIB // 2, align_bytes=64),
            keep.tile([P, HALF], U32, name="w1_codes1", tag=f"zs{first}", align_bytes=64),
        ]
        w1_plane = [keep.tile([P, HALF], U8, name=f"w1_plane{h}", align_bytes=64) for h in range(2)]

        def quantize_w1(h):
            quantize(nc, w1_codes[h][:], w1_plane[h][:], w1_bf[:, halves[h], :])

        quantize_w1(0)
        round_z(LAST, [1])

        quarters = (slice(0, P), slice(P, HALF))
        whole_half = slice(0, HALF)
        for cols in quarters:
            nc.vector.tensor_scalar(z_bf[0][:, cols, LAST], zs[LAST][:, cols], last_gate[:], None, ALU.mult)
        z_codes = [keep.tile([P, HALF], U32, name=f"z_codes{h}", align_bytes=64) for h in range(2)]
        z_plane = [keep.tile([P, HALF], U8, name=f"z_plane{h}", align_bytes=64) for h in range(2)]
        for cols in quarters:
            quantize(nc, z_codes[0][:, cols], z_plane[0][:, cols], z_bf[0][:, cols, :])
        quantize_w1(1)
        quantize(nc, z_codes[1][:], z_plane[1][:], z_bf[1])

        def mix(acc, h, m, cols):
            places = slice(m % 2 * P, (m % 2 + 1) * P)
            multiply(nc, acc, w1_codes[m // 2][:, places], w1_plane[m // 2][:, places], z_codes[h][:, cols], z_plane[h][:, cols])

        copies = (nc.scalar.copy, nc.vector.tensor_copy)
        banks = list(range(BANKS)) + [0]
        for h in range(2):
            for m in range(N // P):
                result = keep.tile([P, HALF], F32, name=f"result{h}{m}", align_bytes=64)
                for cols in quarters if h == m == 0 else [whole_half]:
                    acc = psum.tile([P, cols.stop - cols.start], F32, name="acc", tag=f"bank{banks.pop(0)}")
                    mix(acc[:], h, m, cols)
                    copies[m % 2](result[:, cols], acc[:])
                nc.sync.dma_start(out[m * P : (m + 1) * P, h * HALF : (h + 1) * HALF], result[:])
